import numpy as np
import ml_dtypes


def mxq(x, axis, fmt="e4m3"):
    dtype, down = {"e4m3": (ml_dtypes.float8_e4m3fn, 7), "e5m2": (ml_dtypes.float8_e5m2, 14)}[fmt]
    v = np.moveaxis(np.asarray(x, np.float32).astype(ml_dtypes.bfloat16).astype(np.float64), axis, -1)
    blocks = v.reshape(v.shape[:-1] + (-1, 32))
    amax = np.abs(blocks).max(-1, keepdims=True)
    byte = np.maximum(np.where(amax > 0, np.frexp(amax)[1] - 1 + 127, 0) - down, 1)
    scale = np.exp2(byte - 127.0)
    codes = (blocks / scale).astype(np.float32).astype(dtype).astype(np.float64)
    return np.moveaxis((codes * scale).reshape(v.shape), -1, axis)


WIDE = False


def mx_kscale(k):
    if not WIDE:
        return np.ones(k)
    levels = np.array([10, -10, 5, -5, 0])
    if k % 512:
        return np.exp2(np.random.permutation(np.resize(levels, k // 32))).repeat(32)
    a = np.empty((k // 512, 16))
    for p in range(k // 512):
        a[p, :8] = np.random.permutation(np.resize(levels, 8))
        for g in range(8):
            far = levels[np.abs(levels - a[p, g]) >= 10]
            a[p, g + 8] = far[np.random.randint(len(far))]
    return np.exp2(a.ravel()).repeat(32)


def f64(x):
    return np.asarray(x).astype(np.float64)


def striped(idx):
    return np.tile(idx.reshape(-1, 16).T, (8, 1)).astype(np.uint16)


def unstriped(offs):
    return offs[:16].T.reshape(-1).astype(np.int64)


def pack_weight(w):
    k, n = w.shape
    w = f64(np.asarray(w, np.float32).astype(ml_dtypes.bfloat16)).reshape(k // 32, 32, n)
    amax = np.abs(w).max(1)
    byte = np.clip(np.where(amax > 0, np.frexp(amax)[1] - 1 + 127 - 7, 1), 1, 254)
    scaled = (w * np.exp2(127.0 - byte)[:, None, :]).reshape(k, n).astype(np.float32)
    words = np.ascontiguousarray(scaled.reshape(k // 512, 128, 4, n).transpose(0, 1, 3, 2)).astype(ml_dtypes.float8_e4m3fn).view(np.uint8)
    return words, np.ascontiguousarray(byte.astype(np.uint8).reshape(k // 512, 16, n))


def unpack_weight(words, scales):
    g, p, n, _ = words.shape
    vals = np.ascontiguousarray(words).view(ml_dtypes.float8_e4m3fn).astype(np.float64) * np.repeat(np.exp2(scales.astype(np.float64) - 127.0), 8, axis=1)[..., None]
    return vals.transpose(0, 1, 3, 2).reshape(g * 512, n)


def relu(v):
    return np.maximum(v, 0.0)


K, T, S, D, H, N = 512, 1024, 512, 4, 512, 256
P = 2 ** 7


def setup_inputs():
    n = np.random.standard_normal
    s = mx_kscale(K)[:, None]
    u = mx_kscale(H)
    packed_xT = pack_weight(n((K, T)) * s)
    return {
        "x_words": packed_xT[0],
        "x_scales": packed_xT[1],
        "w1": (n((K, H)) / np.sqrt(K) / s * u).astype(np.float32),
        "w2": (n((H, N)) / np.sqrt(H) / u[:, None]).astype(np.float32),
        "in1": (np.tile((np.arange(S) % 4 >= 1) * 1.0, (P, 1))).astype(np.float32),
        "in2": (np.tile((np.arange(S) % 4 >= 2) * 1.0, (P, 1))).astype(np.float32),
        "offs": striped(np.random.permutation(T)[:S]),
    }


def reference(x_words, x_scales, w1, w2, in1, in2, offs):
    xq = unpack_weight(x_words, x_scales)[:, unstriped(offs)]
    h = relu(mxq(f64(w1), 0, "e4m3").T @ xq)
    y = mxq(f64(w2), 0, "e4m3").T @ mxq(h, 0, "e4m3")
    e0 = np.exp(y)
    e1 = e0 + (np.pad(e0, ((0, 0), (1, 0)))[:, :S]) * f64(in1)[:1]
    e2 = e1 + (np.pad(e1, ((0, 0), (2, 0)))[:, :S]) * f64(in2)[:1]
    gg = np.log(e2) - y
    return gg.reshape(len(gg), -1, D).sum(axis=2)

@@ -1,0 +1,148 @@
+from contextlib import ExitStack
+
+import concourse.mybir as mybir
+
+K, T, S, D, H, N = 512, 1024, 512, 4, 512, 256
+FLOPS = 2 * K * H * S + 2 * H * N * S
+BYTES = K * T + (K // 32) * T + 4 * K * H + 4 * H * N + 2 * 128 * (S // 16) + 4 * N * (S // D)
+
+F32 = mybir.dt.float32
+BF16 = mybir.dt.bfloat16
+I32 = mybir.dt.int32
+U32 = mybir.dt.uint32
+U16 = mybir.dt.uint16
+U8 = mybir.dt.uint8
+FP8X4 = mybir.dt.float8_e4m3fn_x4
+ACT = mybir.ActivationFunctionType
+ALU = mybir.AluOpType
+
+P = 128
+PACK = 4
+CHUNK = 128
+CHUNKS = S // CHUNK
+QPC = CHUNK // D
+MT = N // P
+Q = S // D
+
+
+def tile_picked_ypl_loss_p_kernel(tc, x_words, x_scales, w1, w2, in1, in2, offs, out):
+    nc = tc.nc
+    with ExitStack() as ctx:
+        keep = ctx.enter_context(tc.tile_pool(name="keep", bufs=1))
+        psum = ctx.enter_context(tc.psum_pool(name="psum", bufs=1))
+
+        offsets = keep.tile([P, S // 16], U16, name="offsets")
+        nc.sync.dma_start(offsets[:], offs)
+        words = keep.tile([P, T], U32, name="words", align_bytes=64)
+        nc.sync.dma_start(words[:].bitcast(I32), x_words[0].rearrange("p n t -> p (n t)").bitcast(I32))
+        scales = keep.tile([P, T], U8, name="scales", align_bytes=64)
+        nc.gpsimd.memset(scales[:].bitcast(I32), 0)
+        for q in range(4):
+            nc.sync.dma_start(scales[32 * q : 32 * q + 4, :].bitcast(I32), x_scales[0, 4 * q : 4 * q + 4, :].bitcast(I32))
+
+        w1_rows = w1.rearrange("(p j) c -> p j c", j=PACK)
+        w1_raw = []
+        for half in range(2):
+            raw = keep.tile([P, PACK, H // 2], F32, name=f"w1_raw{half}", align_bytes=64)
+            nc.sync.dma_start(raw[:], w1_rows[:, :, half * (H // 2) : (half + 1) * (H // 2)])
+            w1_raw.append(raw)
+        w2_rows = w2.rearrange("(b t i) n -> t b i n", t=PACK, i=8)
+        w2_raw = keep.tile([P, PACK, N], F32, name="w2_raw", align_bytes=64)
+        for t in range(PACK):
+            nc.sync.dma_start(w2_raw[:, t, :], w2_rows[t])
+
+        x_codes = keep.tile([P, S], U32, name="x_codes", align_bytes=64)
+        x_plane = keep.tile([P, S], U8, name="x_plane", align_bytes=64)
+        nc.vector.tensor_copy(x_codes[:], words[:].indirect(offsets[:]))
+        nc.vector.tensor_copy(x_plane[:], scales[:].indirect(offsets[:]))
+
+        w1_bf = keep.tile([P, PACK, P * PACK], BF16, name="w1_bf", align_bytes=64)
+        dst = w1_bf[:].rearrange("p t (b i j) -> p t b i j", i=8, j=PACK)
+        src = [raw[:].rearrange("p j (b t i) -> p t b i j", t=PACK, i=8) for raw in w1_raw]
+        nc.scalar.copy(dst[:, :, 0:8], src[0])
+        nc.scalar.copy(dst[:, :, 8:11], src[1][:, :, 0:3])
+        nc.vector.tensor_copy(dst[:, :, 11:16], src[1][:, :, 3:8])
+        w1_codes, w1_plane = [], []
+        for t in range(PACK):
+            codes = keep.tile([P, P], U32, name=f"w1_codes{t}", align_bytes=64)
+            plane = keep.tile([P, P], U8, name=f"w1_plane{t}", align_bytes=64)
+            nc.vector.quantize_mx(out=codes[:].bitcast(FP8X4), scales=plane[:], in_=w1_bf[:, t, :])
+            w1_codes.append(codes)
+            w1_plane.append(plane)
+
+        w2_bf = keep.tile([P, N, PACK], BF16, name="w2_bf", align_bytes=64)
+        nc.vector.tensor_copy(w2_bf[:], w2_raw[:].rearrange("p t n -> p n t"))
+        w2_codes = keep.tile([P, N], U32, name="w2_codes", align_bytes=64)
+        w2_plane = keep.tile([P, N], U8, name="w2_plane", align_bytes=64)
+        nc.vector.quantize_mx(out=w2_codes[:].bitcast(FP8X4), scales=w2_plane[:], in_=w2_bf[:].rearrange("p n t -> p (n t)"))
+
+        sums = keep.tile([P, D, MT, CHUNKS, QPC], F32, name="sums", align_bytes=64)
+        score_sum = keep.tile([P, MT, CHUNKS, QPC], F32, name="score_sum", align_bytes=64)
+        h_banks = []
+        for c in range(CHUNKS):
+            cols = slice(c * CHUNK, (c + 1) * CHUNK)
+            h_bank = psum.tile([P, PACK, CHUNK], F32, name=f"h_bank{c}")
+            for t in range(PACK):
+                nc.tensor.matmul_mx(
+                    out=h_bank[:, t, :],
+                    lhsT=w1_codes[t][:].bitcast(FP8X4),
+                    lhsT_scale=w1_plane[t][:],
+                    rhs=x_codes[:, cols].bitcast(FP8X4),
+                    rhs_scale=x_plane[:, cols],
+                    start=True,
+                    stop=True,
+                )
+            h_banks.append(h_bank)
+        y_banks = []
+        for c in range(CHUNKS):
+            h_bank = h_banks[c]
+            h_bf = keep.tile([P, D, QPC, PACK], BF16, name=f"h_bf{c}", align_bytes=64)
+            h_view = h_bank[:].rearrange("p t (v d) -> p d v t", d=D)
+            if c != 2:
+                nc.scalar.activation(h_bf[:], h_view, ACT.Relu)
+            else:
+                nc.vector.tensor_scalar(h_bf[:], h_view, 0.0, None, ALU.max)
+            h_codes = keep.tile([P, CHUNK], U32, name=f"h_codes{c}", align_bytes=64)
+            h_plane = keep.tile([P, CHUNK], U8, name=f"h_plane{c}", align_bytes=64)
+            nc.vector.quantize_mx(out=h_codes[:].bitcast(FP8X4), scales=h_plane[:], in_=h_bf[:].rearrange("p d v t -> p (d v t)"))
+            y_bank = psum.tile([P, MT, CHUNK], F32, name=f"y_bank{c}")
+            for mt in range(MT):
+                nc.tensor.matmul_mx(
+                    out=y_bank[:, mt, :],
+                    lhsT=w2_codes[:, mt * P : (mt + 1) * P].bitcast(FP8X4),
+                    lhsT_scale=w2_plane[:, mt * P : (mt + 1) * P],
+                    rhs=h_codes[:].bitcast(FP8X4),
+                    rhs_scale=h_plane[:],
+                    start=True,
+                    stop=True,
+                )
+            y_view = y_bank[:].rearrange("p m (d v) -> p d m v", d=D)
+            nc.scalar.activation(sums[:, :, :, c, :], y_view, ACT.Exp)
+            y_banks.append(y_bank)
+
+        def score_sums(c):
+            nc.vector.tensor_reduce(
+                score_sum[:, :, c, :],
+                y_banks[c][:].rearrange("p m (d v) -> p m v d", d=D)[:, :, :, 1:D],
+                mybir.AxisListType.X,
+                ALU.add,
+            )
+
+        for c in range(CHUNKS - 1):
+            score_sums(c)
+        flat = sums[:].rearrange("p d m c v -> p d (m c v)")
+        W = MT * Q
+        nc.vector.tensor_tensor(flat[:, 1:4:2, :], flat[:, 0:4:2, :], flat[:, 1:4:2, :], ALU.add)
+        score_sums(CHUNKS - 1)
+        nc.vector.tensor_tensor(flat[:, 2:4, :], flat[:, 1:2, :].to_broadcast([P, 2, W]), flat[:, 2:4, :], ALU.add)
+
+        acc = [score_sum[:, mt].rearrange("p c v -> p (c v)") for mt in range(MT)]
+        for d in range(1, D):
+            logs = keep.tile([P, W], F32, name=f"logs{d}", align_bytes=64)
+            nc.scalar.activation(logs[:], flat[:, d, :], ACT.Ln)
+            for mt in range(MT):
+                total = keep.tile([P, Q], F32, name=f"total{d}_{mt}", align_bytes=64)
+                nc.vector.tensor_tensor(total[:], logs[:, mt * Q : (mt + 1) * Q], acc[mt], ALU.subtract if d == 1 else ALU.add)
+                acc[mt] = total[:]
+        for mt in range(MT):
+            nc.sync.dma_start(out[mt * P : (mt + 1) * P, :], acc[mt])

@@ -29,48 +29,47 @@ def tile_picked_ypl_loss_p_kernel(tc, x_words, x_scales, w1, w2, in1, in2, offs,
     nc = tc.nc
     with ExitStack() as ctx:
         keep = ctx.enter_context(tc.tile_pool(name="keep", bufs=1))
+        stage = ctx.enter_context(tc.tile_pool(name="stage", bufs=1))
         psum = ctx.enter_context(tc.psum_pool(name="psum", bufs=1))
 
         offsets = keep.tile([P, S // 16], U16, name="offsets")
+        w1_rows = w1.rearrange("(p j) c -> p j c", j=PACK)
+        w1_raw = [keep.tile([P, PACK, H // 2], F32, name=f"w1_raw{half}", align_bytes=64) for half in range(2)]
+        nc.sync.dma_start(w1_raw[0][:], w1_rows[:, :, : H // 2])
         nc.sync.dma_start(offsets[:], offs)
-        words = keep.tile([P, T], U32, name="words", align_bytes=64)
-        nc.sync.dma_start(words[:].bitcast(I32), x_words[0].rearrange("p n t -> p (n t)").bitcast(I32))
         scales = keep.tile([P, T], U8, name="scales", align_bytes=64)
         nc.gpsimd.memset(scales[:].bitcast(I32), 0)
         for q in range(4):
             nc.sync.dma_start(scales[32 * q : 32 * q + 4, :].bitcast(I32), x_scales[0, 4 * q : 4 * q + 4, :].bitcast(I32))
-
-        w1_rows = w1.rearrange("(p j) c -> p j c", j=PACK)
-        w1_raw = []
-        for half in range(2):
-            raw = keep.tile([P, PACK, H // 2], F32, name=f"w1_raw{half}", align_bytes=64)
-            nc.sync.dma_start(raw[:], w1_rows[:, :, half * (H // 2) : (half + 1) * (H // 2)])
-            w1_raw.append(raw)
+        nc.sync.dma_start(w1_raw[1][:], w1_rows[:, :, H // 2 :])
+        words = keep.tile([P, T], U32, name="words", align_bytes=64)
+        nc.sync.dma_start(words[:].bitcast(I32), x_words[0].rearrange("p n t -> p (n t)").bitcast(I32))
         w2_rows = w2.rearrange("(b t i) n -> t b i n", t=PACK, i=8)
         w2_raw = keep.tile([P, PACK, N], F32, name="w2_raw", align_bytes=64)
         for t in range(PACK):
             nc.sync.dma_start(w2_raw[:, t, :], w2_rows[t])
 
-        x_codes = keep.tile([P, S], U32, name="x_codes", align_bytes=64)
         x_plane = keep.tile([P, S], U8, name="x_plane", align_bytes=64)
-        nc.vector.tensor_copy(x_codes[:], words[:].indirect(offsets[:]))
         nc.vector.tensor_copy(x_plane[:], scales[:].indirect(offsets[:]))
 
-        w1_bf = keep.tile([P, PACK, P * PACK], BF16, name="w1_bf", align_bytes=64)
+        w1_bf = stage.tile([P, PACK, P * PACK], BF16, name="w1_bf", align_bytes=64, offset=0)
         dst = w1_bf[:].rearrange("p t (b i j) -> p t b i j", i=8, j=PACK)
         src = [raw[:].rearrange("p j (b t i) -> p t b i j", t=PACK, i=8) for raw in w1_raw]
         nc.scalar.copy(dst[:, :, 0:8], src[0])
-        nc.scalar.copy(dst[:, :, 8:11], src[1][:, :, 0:3])
-        nc.vector.tensor_copy(dst[:, :, 11:16], src[1][:, :, 3:8])
-        w1_codes, w1_plane = [], []
-        for t in range(PACK):
-            codes = keep.tile([P, P], U32, name=f"w1_codes{t}", align_bytes=64)
-            plane = keep.tile([P, P], U8, name=f"w1_plane{t}", align_bytes=64)
-            nc.vector.quantize_mx(out=codes[:].bitcast(FP8X4), scales=plane[:], in_=w1_bf[:, t, :])
-            w1_codes.append(codes)
-            w1_plane.append(plane)
+        nc.scalar.copy(dst[:, :, 8:10], src[1][:, :, 0:2])
+        nc.vector.tensor_copy(dst[:, :, 10:16], src[1][:, :, 2:8])
+        w1_codes = keep.tile([P, H], U32, name="w1_codes", align_bytes=64)
+        w1_plane = keep.tile([P, H], U8, name="w1_plane", align_bytes=64)
+        nc.vector.quantize_mx(out=w1_codes[:].bitcast(FP8X4), scales=w1_plane[:], in_=w1_bf[:].rearrange("p t n -> p (t n)"))
 
-        w2_bf = keep.tile([P, N, PACK], BF16, name="w2_bf", align_bytes=64)
+        x_codes = stage.tile([P, S], U32, name="x_codes", align_bytes=64, offset=0)
+        for first, last in ((0, 1), (1, 2), (2, 4)):
+            nc.vector.tensor_copy(
+                x_codes[:, first * CHUNK : last * CHUNK],
+                words[:].indirect(offsets[:, first * (CHUNK // 16) : last * (CHUNK // 16)]),
+            )
+
+        w2_bf = stage.tile([P, N, PACK], BF16, name="w2_bf", align_bytes=64, offset=2048)
         nc.vector.tensor_copy(w2_bf[:], w2_raw[:].rearrange("p t n -> p n t"))
         w2_codes = keep.tile([P, N], U32, name="w2_codes", align_bytes=64)
         w2_plane = keep.tile([P, N], U8, name="w2_plane", align_bytes=64)
@@ -85,8 +84,8 @@ def tile_picked_ypl_loss_p_kernel(tc, x_words, x_scales, w1, w2, in1, in2, offs,
             for t in range(PACK):
                 nc.tensor.matmul_mx(
                     out=h_bank[:, t, :],
-                    lhsT=w1_codes[t][:].bitcast(FP8X4),
-                    lhsT_scale=w1_plane[t][:],
+                    lhsT=w1_codes[:, t * P : (t + 1) * P].bitcast(FP8X4),
+                    lhsT_scale=w1_plane[:, t * P : (t + 1) * P],
                     rhs=x_codes[:, cols].bitcast(FP8X4),
                     rhs_scale=x_plane[:, cols],
                     start=True,
@@ -94,24 +93,22 @@ def tile_picked_ypl_loss_p_kernel(tc, x_words, x_scales, w1, w2, in1, in2, offs,
                 )
             h_banks.append(h_bank)
         y_banks = []
+        h_codes = stage.tile([P, S], U32, name="h_codes", align_bytes=64, offset=2048)
         for c in range(CHUNKS):
             h_bank = h_banks[c]
             h_bf = keep.tile([P, D, QPC, PACK], BF16, name=f"h_bf{c}", align_bytes=64)
             h_view = h_bank[:].rearrange("p t (v d) -> p d v t", d=D)
-            if c != 2:
-                nc.scalar.activation(h_bf[:], h_view, ACT.Relu)
-            else:
-                nc.vector.tensor_scalar(h_bf[:], h_view, 0.0, None, ALU.max)
-            h_codes = keep.tile([P, CHUNK], U32, name=f"h_codes{c}", align_bytes=64)
+            nc.scalar.activation(h_bf[:], h_view, ACT.Relu)
+            cols = slice(c * CHUNK, (c + 1) * CHUNK)
             h_plane = keep.tile([P, CHUNK], U8, name=f"h_plane{c}", align_bytes=64)
-            nc.vector.quantize_mx(out=h_codes[:].bitcast(FP8X4), scales=h_plane[:], in_=h_bf[:].rearrange("p d v t -> p (d v t)"))
+            nc.vector.quantize_mx(out=h_codes[:, cols].bitcast(FP8X4), scales=h_plane[:], in_=h_bf[:].rearrange("p d v t -> p (d v t)"))
             y_bank = psum.tile([P, MT, CHUNK], F32, name=f"y_bank{c}")
             for mt in range(MT):
                 nc.tensor.matmul_mx(
                     out=y_bank[:, mt, :],
                     lhsT=w2_codes[:, mt * P : (mt + 1) * P].bitcast(FP8X4),
                     lhsT_scale=w2_plane[:, mt * P : (mt + 1) * P],
-                    rhs=h_codes[:].bitcast(FP8X4),
+                    rhs=h_codes[:, cols].bitcast(FP8X4),
                     rhs_scale=h_plane[:],
                     start=True,
                     stop=True,

@@ -52,22 +52,33 @@ def tile_picked_ypl_loss_p_kernel(tc, x_words, x_scales, w1, w2, in1, in2, offs,
         x_plane = keep.tile([P, S], U8, name="x_plane", align_bytes=64)
         nc.vector.tensor_copy(x_plane[:], scales[:].indirect(offsets[:]))
 
-        w1_bf = stage.tile([P, PACK, P * PACK], BF16, name="w1_bf", align_bytes=64, offset=0)
-        dst = w1_bf[:].rearrange("p t (b i j) -> p t b i j", i=8, j=PACK)
+        w1_bf = [stage.tile([P, 2, P * PACK], BF16, name=f"w1_bf{u}", align_bytes=64, offset=2048 * u) for u in range(2)]
+        dst = [bf[:].rearrange("p t (b i j) -> p t b i j", i=8, j=PACK) for bf in w1_bf]
         src = [raw[:].rearrange("p j (b t i) -> p t b i j", t=PACK, i=8) for raw in w1_raw]
-        nc.scalar.copy(dst[:, :, 0:8], src[0])
-        nc.scalar.copy(dst[:, :, 8:10], src[1][:, :, 0:2])
-        nc.vector.tensor_copy(dst[:, :, 10:16], src[1][:, :, 2:8])
+        nc.scalar.copy(dst[0][:, :, 0:8], src[0][:, 0:2])
+        nc.scalar.copy(dst[1][:, :, 0:8], src[0][:, 2:4])
+        nc.vector.tensor_copy(dst[0][:, :, 8:16], src[1][:, 0:2])
+        nc.scalar.copy(dst[1][:, :, 8:12], src[1][:, 2:4, 0:4])
+        nc.vector.tensor_copy(dst[1][:, :, 12:16], src[1][:, 2:4, 4:8])
         w1_codes = keep.tile([P, H], U32, name="w1_codes", align_bytes=64)
         w1_plane = keep.tile([P, H], U8, name="w1_plane", align_bytes=64)
-        nc.vector.quantize_mx(out=w1_codes[:].bitcast(FP8X4), scales=w1_plane[:], in_=w1_bf[:].rearrange("p t n -> p (t n)"))
-
         x_codes = stage.tile([P, S], U32, name="x_codes", align_bytes=64, offset=0)
-        for first, last in ((0, 1), (1, 2), (2, 4)):
+
+        def quantize_w1(u):
+            cols = slice(2 * u * P, 2 * (u + 1) * P)
+            nc.vector.quantize_mx(out=w1_codes[:, cols].bitcast(FP8X4), scales=w1_plane[:, cols], in_=w1_bf[u][:].rearrange("p t n -> p (t n)"))
+
+        def gather_words(first, last):
             nc.vector.tensor_copy(
                 x_codes[:, first * CHUNK : last * CHUNK],
                 words[:].indirect(offsets[:, first * (CHUNK // 16) : last * (CHUNK // 16)]),
             )
+
+        quantize_w1(0)
+        gather_words(0, 1)
+        quantize_w1(1)
+        gather_words(1, 2)
+        gather_words(2, 4)
 
         w2_bf = stage.tile([P, N, PACK], BF16, name="w2_bf", align_bytes=64, offset=2048)
         nc.vector.tensor_copy(w2_bf[:], w2_raw[:].rearrange("p t n -> p n t"))
@@ -93,12 +104,16 @@ def tile_picked_ypl_loss_p_kernel(tc, x_words, x_scales, w1, w2, in1, in2, offs,
                 )
             h_banks.append(h_bank)
         y_banks = []
-        h_codes = stage.tile([P, S], U32, name="h_codes", align_bytes=64, offset=2048)
+        h_codes = stage.tile([P, S], U32, name="h_codes", align_bytes=64, offset=3072)
         for c in range(CHUNKS):
             h_bank = h_banks[c]
-            h_bf = keep.tile([P, D, QPC, PACK], BF16, name=f"h_bf{c}", align_bytes=64)
             h_view = h_bank[:].rearrange("p t (v d) -> p d v t", d=D)
-            nc.scalar.activation(h_bf[:], h_view, ACT.Relu)
+            if c == 2:
+                h_bf = stage.tile([P, D, QPC, PACK], BF16, name="h_bf_vector", align_bytes=64, offset=2048)
+                nc.vector.tensor_scalar(h_bf[:], h_view, 0.0, None, ALU.max)
+            else:
+                h_bf = keep.tile([P, D, QPC, PACK], BF16, name=f"h_bf{c}", align_bytes=64)
+                nc.scalar.activation(h_bf[:], h_view, ACT.Relu)
             cols = slice(c * CHUNK, (c + 1) * CHUNK)
             h_plane = keep.tile([P, CHUNK], U8, name=f"h_plane{c}", align_bytes=64)
             nc.vector.quantize_mx(out=h_codes[:, cols].bitcast(FP8X4), scales=h_plane[:], in_=h_bf[:].rearrange("p d v t -> p (d v t)"))
@@ -125,13 +140,23 @@ def tile_picked_ypl_loss_p_kernel(tc, x_words, x_scales, w1, w2, in1, in2, offs,
                 ALU.add,
             )
 
-        for c in range(CHUNKS - 1):
-            score_sums(c)
+        rows = sums[:].rearrange("p d m c v -> p d m (c v)")
+
+        def add_pairs(v):
+            nc.vector.tensor_tensor(rows[:, 1:4:2, :, v], rows[:, 0:4:2, :, v], rows[:, 1:4:2, :, v], ALU.add)
+
+        def add_first_two(v):
+            first_two = rows[:, 1:2, :, v].to_broadcast([P, 2, MT, v.stop - v.start])
+            nc.vector.tensor_tensor(rows[:, 2:4, :, v], first_two, rows[:, 2:4, :, v], ALU.add)
+
+        for half in range(2):
+            queries = slice(half * Q // 2, (half + 1) * Q // 2)
+            score_sums(2 * half)
+            add_pairs(queries)
+            score_sums(2 * half + 1)
+            add_first_two(queries)
         flat = sums[:].rearrange("p d m c v -> p d (m c v)")
         W = MT * Q
-        nc.vector.tensor_tensor(flat[:, 1:4:2, :], flat[:, 0:4:2, :], flat[:, 1:4:2, :], ALU.add)
-        score_sums(CHUNKS - 1)
-        nc.vector.tensor_tensor(flat[:, 2:4, :], flat[:, 1:2, :].to_broadcast([P, 2, W]), flat[:, 2:4, :], ALU.add)
 
         acc = [score_sum[:, mt].rearrange("p c v -> p (c v)") for mt in range(MT)]
         for d in range(1, D):

@@ -88,6 +88,17 @@ def tile_picked_ypl_loss_p_kernel(tc, x_words, x_scales, w1, w2, in1, in2, offs,
 
         sums = keep.tile([P, D, MT, CHUNKS, QPC], F32, name="sums", align_bytes=64)
         score_sum = keep.tile([P, MT, CHUNKS, QPC], F32, name="score_sum", align_bytes=64)
+        warm = psum.tile([P, MT, CHUNK], F32, name="warm", tag="y_bank3")
+        for width in (2 * P, 2 * P, P):
+            nc.tensor.matmul_mx(
+                out=warm[:].rearrange("p m n -> p (m n)")[:, :width],
+                lhsT=w1_codes[:, :P].bitcast(FP8X4),
+                lhsT_scale=w1_plane[:, :P],
+                rhs=w1_codes[:, :width].bitcast(FP8X4),
+                rhs_scale=w1_plane[:, :width],
+                start=True,
+                stop=True,
+            )
         h_banks = []
         for c in range(CHUNKS):
             cols = slice(c * CHUNK, (c + 1) * CHUNK)
@@ -117,7 +128,7 @@ def tile_picked_ypl_loss_p_kernel(tc, x_words, x_scales, w1, w2, in1, in2, offs,
             cols = slice(c * CHUNK, (c + 1) * CHUNK)
             h_plane = keep.tile([P, CHUNK], U8, name=f"h_plane{c}", align_bytes=64)
             nc.vector.quantize_mx(out=h_codes[:, cols].bitcast(FP8X4), scales=h_plane[:], in_=h_bf[:].rearrange("p d v t -> p (d v t)"))
-            y_bank = psum.tile([P, MT, CHUNK], F32, name=f"y_bank{c}")
+            y_bank = psum.tile([P, MT, CHUNK], F32, name=f"y_bank{c}", tag=f"y_bank{c}")
             for mt in range(MT):
                 nc.tensor.matmul_mx(
                     out=y_bank[:, mt, :],

@@ -1,3 +1,4 @@
+import math
 from contextlib import ExitStack
 
 import concourse.mybir as mybir
@@ -20,9 +21,22 @@ P = 128
 PACK = 4
 CHUNK = 128
 CHUNKS = S // CHUNK
-QPC = CHUNK // D
-MT = N // P
-Q = S // D
+CHUNK_QUERIES = CHUNK // D
+QUERIES = S // D
+OUT_TILES = N // P
+HALF_GROUPS = H // 2 // 8
+LAST = CHUNKS - 1
+EXPONENT_FIELD = 0x7F800000
+LN2 = math.log(2.0)
+VECTOR_CHUNK = 2
+
+W1_BF_AT = (0, 2048)
+X_CODES_AT = (W1_BF_AT[1], W1_BF_AT[0], W1_BF_AT[0] + 512, W1_BF_AT[0] + 1024)
+W2_BF_AT = 4096
+W2_RAW_AT = 8192
+H_CODES_AT = (W2_RAW_AT, W2_BF_AT + 1024, W2_BF_AT + 2048, W2_BF_AT + 1536)
+W1_CODES_AT = 14336
+SCALES_AT = W1_CODES_AT - 512
 
 
 def tile_picked_ypl_loss_p_kernel(tc, x_words, x_scales, w1, w2, in1, in2, offs, out):
@@ -35,147 +49,153 @@ def tile_picked_ypl_loss_p_kernel(tc, x_words, x_scales, w1, w2, in1, in2, offs,
         offsets = keep.tile([P, S // 16], U16, name="offsets")
         w1_rows = w1.rearrange("(p j) c -> p j c", j=PACK)
         w1_raw = [keep.tile([P, PACK, H // 2], F32, name=f"w1_raw{half}", align_bytes=64) for half in range(2)]
+        scales = stage.tile([P, T], U8, name="scales", align_bytes=64, offset=SCALES_AT)
+        nc.vector.memset(scales[:].bitcast(I32), 0)
+        words = keep.tile([P, T], U32, name="words", align_bytes=64)
+        w2_rows = w2.rearrange("(g u i e) n -> u g i (e n)", u=2, i=2, e=2)
+        w2_raw = stage.tile([P, PACK, N], F32, name="w2_raw", align_bytes=64, offset=W2_RAW_AT)
+
         nc.sync.dma_start(w1_raw[0][:], w1_rows[:, :, : H // 2])
         nc.sync.dma_start(offsets[:], offs)
-        scales = keep.tile([P, T], U8, name="scales", align_bytes=64)
-        nc.gpsimd.memset(scales[:].bitcast(I32), 0)
         for q in range(4):
             nc.sync.dma_start(scales[32 * q : 32 * q + 4, :].bitcast(I32), x_scales[0, 4 * q : 4 * q + 4, :].bitcast(I32))
         nc.sync.dma_start(w1_raw[1][:], w1_rows[:, :, H // 2 :])
-        words = keep.tile([P, T], U32, name="words", align_bytes=64)
         nc.sync.dma_start(words[:].bitcast(I32), x_words[0].rearrange("p n t -> p (n t)").bitcast(I32))
-        w2_rows = w2.rearrange("(b t i) n -> t b i n", t=PACK, i=8)
-        w2_raw = keep.tile([P, PACK, N], F32, name="w2_raw", align_bytes=64)
-        for t in range(PACK):
-            nc.sync.dma_start(w2_raw[:, t, :], w2_rows[t])
+        for u in range(2):
+            nc.sync.dma_start(w2_raw[:, 2 * u : 2 * u + 2, :].rearrange("p e n -> p (e n)"), w2_rows[u])
 
-        x_plane = keep.tile([P, S], U8, name="x_plane", align_bytes=64)
-        nc.vector.tensor_copy(x_plane[:], scales[:].indirect(offsets[:]))
+        x_scales_picked = keep.tile([P, S], U8, name="x_scales_picked", align_bytes=64)
+        nc.vector.tensor_copy(x_scales_picked[:], scales[:].indirect(offsets[:]))
 
-        w1_bf = [stage.tile([P, 2, P * PACK], BF16, name=f"w1_bf{u}", align_bytes=64, offset=2048 * u) for u in range(2)]
-        dst = [bf[:].rearrange("p t (b i j) -> p t b i j", i=8, j=PACK) for bf in w1_bf]
-        src = [raw[:].rearrange("p j (b t i) -> p t b i j", t=PACK, i=8) for raw in w1_raw]
-        nc.scalar.copy(dst[0][:, :, 0:8], src[0][:, 0:2])
-        nc.scalar.copy(dst[1][:, :, 0:8], src[0][:, 2:4])
-        nc.vector.tensor_copy(dst[0][:, :, 8:16], src[1][:, 0:2])
-        nc.scalar.copy(dst[1][:, :, 8:12], src[1][:, 2:4, 0:4])
-        nc.vector.tensor_copy(dst[1][:, :, 12:16], src[1][:, 2:4, 4:8])
-        w1_codes = keep.tile([P, H], U32, name="w1_codes", align_bytes=64)
-        w1_plane = keep.tile([P, H], U8, name="w1_plane", align_bytes=64)
-        x_codes = stage.tile([P, S], U32, name="x_codes", align_bytes=64, offset=0)
+        w1_codes = stage.tile([P, H], U32, name="w1_codes", align_bytes=64, offset=W1_CODES_AT)
+        w1_scales = keep.tile([P, H], U8, name="w1_scales", align_bytes=64)
+        w1_bf = [stage.tile([P, 2, P * PACK], BF16, name=f"w1_bf{u}", align_bytes=64, offset=W1_BF_AT[u]) for u in range(2)]
+        for half in range(2):
+            columns = w1_raw[half][:].rearrange("p j (g u i e) -> p u g j i e", u=2, i=2, e=2)
+            for u in (1, 0):
+                dealt = w1_bf[u][:].rearrange("p e (g i j) -> p g j i e", i=2, j=PACK)[:, half * HALF_GROUPS : (half + 1) * HALF_GROUPS]
+                if half == 1 and u == 1:
+                    nc.vector.tensor_copy(dealt, columns[:, u])
+                else:
+                    nc.scalar.copy(dealt, columns[:, u])
+        x_codes = [stage.tile([P, CHUNK], U32, name=f"x_codes{c}", align_bytes=64, offset=X_CODES_AT[c]) for c in range(CHUNKS)]
 
         def quantize_w1(u):
             cols = slice(2 * u * P, 2 * (u + 1) * P)
-            nc.vector.quantize_mx(out=w1_codes[:, cols].bitcast(FP8X4), scales=w1_plane[:, cols], in_=w1_bf[u][:].rearrange("p t n -> p (t n)"))
+            nc.vector.quantize_mx(out=w1_codes[:, cols].bitcast(FP8X4), scales=w1_scales[:, cols], in_=w1_bf[u][:].rearrange("p e n -> p (e n)"))
 
-        def gather_words(first, last):
-            nc.vector.tensor_copy(
-                x_codes[:, first * CHUNK : last * CHUNK],
-                words[:].indirect(offsets[:, first * (CHUNK // 16) : last * (CHUNK // 16)]),
-            )
+        def gather_words(c):
+            nc.vector.tensor_copy(x_codes[c][:], words[:].indirect(offsets[:, c * (CHUNK // 16) : (c + 1) * (CHUNK // 16)]))
 
-        quantize_w1(0)
-        gather_words(0, 1)
         quantize_w1(1)
-        gather_words(1, 2)
-        gather_words(2, 4)
+        gather_words(0)
+        quantize_w1(0)
+        for c in range(1, CHUNKS):
+            gather_words(c)
 
-        w2_bf = stage.tile([P, N, PACK], BF16, name="w2_bf", align_bytes=64, offset=2048)
-        nc.vector.tensor_copy(w2_bf[:], w2_raw[:].rearrange("p t n -> p n t"))
+        w2_bf = stage.tile([P, N, PACK], BF16, name="w2_bf", align_bytes=64, offset=W2_BF_AT)
+        nc.vector.tensor_copy(w2_bf[:].rearrange("p (a l) t -> p a t l", l=4), w2_raw[:].rearrange("p t (a l) -> p a t l", l=4))
         w2_codes = keep.tile([P, N], U32, name="w2_codes", align_bytes=64)
-        w2_plane = keep.tile([P, N], U8, name="w2_plane", align_bytes=64)
-        nc.vector.quantize_mx(out=w2_codes[:].bitcast(FP8X4), scales=w2_plane[:], in_=w2_bf[:].rearrange("p n t -> p (n t)"))
+        w2_scales = keep.tile([P, N], U8, name="w2_scales", align_bytes=64)
+        nc.vector.quantize_mx(out=w2_codes[:].bitcast(FP8X4), scales=w2_scales[:], in_=w2_bf[:].rearrange("p n t -> p (n t)"))
 
-        sums = keep.tile([P, D, MT, CHUNKS, QPC], F32, name="sums", align_bytes=64)
-        score_sum = keep.tile([P, MT, CHUNKS, QPC], F32, name="score_sum", align_bytes=64)
-        warm = psum.tile([P, MT, CHUNK], F32, name="warm", tag="y_bank3")
-        for width in (2 * P, 2 * P, P):
-            nc.tensor.matmul_mx(
-                out=warm[:].rearrange("p m n -> p (m n)")[:, :width],
-                lhsT=w1_codes[:, :P].bitcast(FP8X4),
-                lhsT_scale=w1_plane[:, :P],
-                rhs=w1_codes[:, :width].bitcast(FP8X4),
-                rhs_scale=w1_plane[:, :width],
-                start=True,
-                stop=True,
-            )
+        sums = keep.tile([P, D, OUT_TILES, CHUNKS, CHUNK_QUERIES], F32, name="sums", align_bytes=64)
+        score_sum = keep.tile([P, OUT_TILES, CHUNKS, CHUNK_QUERIES], F32, name="score_sum", align_bytes=64)
+
         h_banks = []
         for c in range(CHUNKS):
             cols = slice(c * CHUNK, (c + 1) * CHUNK)
-            h_bank = psum.tile([P, PACK, CHUNK], F32, name=f"h_bank{c}")
-            for t in range(PACK):
+            h_bank = psum.tile([P, PACK, CHUNK], F32, name=f"h_bank{c}", tag=f"h_bank{c}")
+            for t in (2, 3, 0, 1):
                 nc.tensor.matmul_mx(
                     out=h_bank[:, t, :],
                     lhsT=w1_codes[:, t * P : (t + 1) * P].bitcast(FP8X4),
-                    lhsT_scale=w1_plane[:, t * P : (t + 1) * P],
-                    rhs=x_codes[:, cols].bitcast(FP8X4),
-                    rhs_scale=x_plane[:, cols],
+                    lhsT_scale=w1_scales[:, t * P : (t + 1) * P],
+                    rhs=x_codes[c][:].bitcast(FP8X4),
+                    rhs_scale=x_scales_picked[:, cols],
                     start=True,
                     stop=True,
                 )
             h_banks.append(h_bank)
-        y_banks = []
-        h_codes = stage.tile([P, S], U32, name="h_codes", align_bytes=64, offset=3072)
-        for c in range(CHUNKS):
-            h_bank = h_banks[c]
-            h_view = h_bank[:].rearrange("p t (v d) -> p d v t", d=D)
-            if c == 2:
-                h_bf = stage.tile([P, D, QPC, PACK], BF16, name="h_bf_vector", align_bytes=64, offset=2048)
-                nc.vector.tensor_scalar(h_bf[:], h_view, 0.0, None, ALU.max)
-            else:
-                h_bf = keep.tile([P, D, QPC, PACK], BF16, name=f"h_bf{c}", align_bytes=64)
-                nc.scalar.activation(h_bf[:], h_view, ACT.Relu)
-            cols = slice(c * CHUNK, (c + 1) * CHUNK)
-            h_plane = keep.tile([P, CHUNK], U8, name=f"h_plane{c}", align_bytes=64)
-            nc.vector.quantize_mx(out=h_codes[:, cols].bitcast(FP8X4), scales=h_plane[:], in_=h_bf[:].rearrange("p d v t -> p (d v t)"))
-            y_bank = psum.tile([P, MT, CHUNK], F32, name=f"y_bank{c}", tag=f"y_bank{c}")
-            for mt in range(MT):
+
+        h_view = [bank[:].rearrange("p t (v d) -> p d v t", d=D) for bank in h_banks]
+        h_bf = [keep.tile([P, D, CHUNK_QUERIES, PACK], BF16, name=f"h_bf{c}", align_bytes=64) for c in range(CHUNKS - 1)]
+        h_bf.insert(VECTOR_CHUNK, stage.tile([P, D, CHUNK_QUERIES, PACK], BF16, name="h_bf_vector", align_bytes=64, offset=W2_BF_AT))
+        halves = [slice(0, D // 2), slice(D // 2, D)]
+        for c in range(LAST):
+            if c != VECTOR_CHUNK:
+                nc.scalar.activation(h_bf[c][:], h_view[c], ACT.Relu)
+        for part in halves:
+            nc.scalar.activation(h_bf[LAST][:, part], h_view[LAST][:, part], ACT.Relu)
+        h_codes = [stage.tile([P, CHUNK], U32, name=f"h_codes{c}", align_bytes=64, offset=H_CODES_AT[c]) for c in range(CHUNKS)]
+
+        def second_product(c, part, bank_tag):
+            cols = slice(part.start * CHUNK_QUERIES, part.stop * CHUNK_QUERIES)
+            width = cols.stop - cols.start
+            h_scales = keep.tile([P, width], U8, name=f"h_scales{c}_{part.start}", align_bytes=64)
+            nc.vector.quantize_mx(out=h_codes[c][:, cols].bitcast(FP8X4), scales=h_scales[:], in_=h_bf[c][:, part].rearrange("p d v t -> p (d v t)"))
+            y_bank = psum.tile([P, OUT_TILES, width], F32, name=f"y_bank{c}_{part.start}", tag=bank_tag)
+            for m in range(OUT_TILES):
                 nc.tensor.matmul_mx(
-                    out=y_bank[:, mt, :],
-                    lhsT=w2_codes[:, mt * P : (mt + 1) * P].bitcast(FP8X4),
-                    lhsT_scale=w2_plane[:, mt * P : (mt + 1) * P],
-                    rhs=h_codes[:, cols].bitcast(FP8X4),
-                    rhs_scale=h_plane[:],
+                    out=y_bank[:, m, :],
+                    lhsT=w2_codes[:, m * P : (m + 1) * P].bitcast(FP8X4),
+                    lhsT_scale=w2_scales[:, m * P : (m + 1) * P],
+                    rhs=h_codes[c][:, cols].bitcast(FP8X4),
+                    rhs_scale=h_scales[:],
                     start=True,
                     stop=True,
                 )
-            y_view = y_bank[:].rearrange("p m (d v) -> p d m v", d=D)
-            nc.scalar.activation(sums[:, :, :, c, :], y_view, ACT.Exp)
-            y_banks.append(y_bank)
+            scores = y_bank[:].rearrange("p m (d v) -> p m d v", v=CHUNK_QUERIES)
+            nc.scalar.activation(sums[:, part, :, c, :], scores.rearrange("p m d v -> p d m v"), ACT.Exp)
+            return scores
+
+        whole = slice(0, D)
+        chunk_scores = [second_product(0, whole, "y_bank0")]
+        nc.vector.tensor_scalar(h_bf[VECTOR_CHUNK][:], h_view[VECTOR_CHUNK], 0.0, None, ALU.max)
+        chunk_scores.extend([second_product(c, whole, f"y_bank{c}") for c in range(1, LAST)])
+        half_scores = [second_product(LAST, part, tag) for part, tag in zip(halves, (f"y_bank{LAST}", "h_bank0"))]
 
         def score_sums(c):
-            nc.vector.tensor_reduce(
-                score_sum[:, :, c, :],
-                y_banks[c][:].rearrange("p m (d v) -> p m v d", d=D)[:, :, :, 1:D],
-                mybir.AxisListType.X,
-                ALU.add,
-            )
+            nc.vector.tensor_reduce(score_sum[:, :, c, :], chunk_scores[c].rearrange("p m d v -> p m v d")[:, :, :, 1:D], mybir.AxisListType.X, ALU.add)
 
-        rows = sums[:].rearrange("p d m c v -> p d m (c v)")
+        places = sums[:].rearrange("p d m c v -> p d m (c v)")
 
-        def add_pairs(v):
-            nc.vector.tensor_tensor(rows[:, 1:4:2, :, v], rows[:, 0:4:2, :, v], rows[:, 1:4:2, :, v], ALU.add)
+        def add_place(d, queries):
+            nc.vector.tensor_tensor(places[:, d, :, queries], places[:, d - 1, :, queries], places[:, d, :, queries], ALU.add)
 
-        def add_first_two(v):
-            first_two = rows[:, 1:2, :, v].to_broadcast([P, 2, MT, v.stop - v.start])
-            nc.vector.tensor_tensor(rows[:, 2:4, :, v], first_two, rows[:, 2:4, :, v], ALU.add)
+        factor = keep.tile([P, OUT_TILES, QUERIES], F32, name="factor", align_bytes=64)
+        product = keep.tile([P, OUT_TILES, QUERIES], F32, name="product", align_bytes=64)
+        offset = keep.tile([P, OUT_TILES, QUERIES], F32, name="offset", align_bytes=64)
+        early, late = slice(0, QUERIES // 2), slice(QUERIES // 2, QUERIES)
+        add_place(1, early)
+        score_sums(0)
+        add_place(2, early)
+        score_sums(1)
+        add_place(1, late)
+        add_place(3, early)
+        nc.vector.tensor_scalar(factor[:].bitcast(I32), places[:, 1].bitcast(I32), EXPONENT_FIELD, EXPONENT_FIELD, ALU.bitwise_and, ALU.bitwise_xor)
+        add_place(2, late)
+        nc.vector.tensor_tensor(places[:, 0], places[:, 1], factor[:], ALU.mult)
+        add_place(3, late)
+        nc.vector.tensor_tensor(product[:], places[:, 0], places[:, 2], ALU.mult)
+        score_sums(2)
+        upper_scores = keep.tile([P, OUT_TILES, CHUNK_QUERIES], F32, name="upper_scores", align_bytes=64)
+        nc.vector.tensor_reduce(upper_scores[:], half_scores[1].rearrange("p m d v -> p m v d"), mybir.AxisListType.X, ALU.add)
+        nc.vector.tensor_tensor(score_sum[:, :, LAST, :], half_scores[0][:, :, 1, :], upper_scores[:], ALU.add)
+        nc.vector.scalar_tensor_tensor(
+            offset[:], factor[:].bitcast(I32), -LN2 / 2**23, score_sum[:].rearrange("p m c v -> p m (c v)"), ALU.mult, ALU.subtract
+        )
 
-        for half in range(2):
-            queries = slice(half * Q // 2, (half + 1) * Q // 2)
-            score_sums(2 * half)
-            add_pairs(queries)
-            score_sums(2 * half + 1)
-            add_first_two(queries)
-        flat = sums[:].rearrange("p d m c v -> p d (m c v)")
-        W = MT * Q
-
-        acc = [score_sum[:, mt].rearrange("p c v -> p (c v)") for mt in range(MT)]
-        for d in range(1, D):
-            logs = keep.tile([P, W], F32, name=f"logs{d}", align_bytes=64)
-            nc.scalar.activation(logs[:], flat[:, d, :], ACT.Ln)
-            for mt in range(MT):
-                total = keep.tile([P, Q], F32, name=f"total{d}_{mt}", align_bytes=64)
-                nc.vector.tensor_tensor(total[:], logs[:, mt * Q : (mt + 1) * Q], acc[mt], ALU.subtract if d == 1 else ALU.add)
-                acc[mt] = total[:]
-        for mt in range(MT):
-            nc.sync.dma_start(out[mt * P : (mt + 1) * P, :], acc[mt])
+        partial = []
+        for m in range(OUT_TILES):
+            log_last = keep.tile([P, QUERIES], F32, name=f"log_last{m}", align_bytes=64)
+            nc.scalar.activation(log_last[:], places[:, 3, m, :], ACT.Ln)
+            rest = keep.tile([P, QUERIES], F32, name=f"rest{m}", align_bytes=64)
+            nc.vector.scalar_tensor_tensor(rest[:], log_last[:], 128 * LN2, offset[:, m], ALU.add, ALU.add)
+            partial.append(rest)
+        for m in range(OUT_TILES):
+            log_product = keep.tile([P, QUERIES], F32, name=f"log_product{m}", align_bytes=64)
+            nc.scalar.activation(log_product[:], product[:, m], ACT.Ln, scale=0.5)
+            result = keep.tile([P, QUERIES], F32, name=f"result{m}", align_bytes=64)
+            nc.vector.tensor_tensor(result[:], log_product[:], partial[m][:], ALU.add)
+            nc.sync.dma_start(out[m * P : (m + 1) * P, :], result[:])

@@ -48,18 +48,18 @@ def tile_picked_ypl_loss_p_kernel(tc, x_words, x_scales, w1, w2, in1, in2, offs,
 
         offsets = keep.tile([P, S // 16], U16, name="offsets")
         w1_rows = w1.rearrange("(p j) c -> p j c", j=PACK)
-        w1_raw = [keep.tile([P, PACK, H // 2], F32, name=f"w1_raw{half}", align_bytes=64) for half in range(2)]
+        w1_raw = [keep.tile([P, 2, H], F32, name=f"w1_raw{half}", align_bytes=64) for half in range(2)]
         scales = stage.tile([P, T], U8, name="scales", align_bytes=64, offset=SCALES_AT)
         nc.vector.memset(scales[:].bitcast(I32), 0)
         words = keep.tile([P, T], U32, name="words", align_bytes=64)
         w2_rows = w2.rearrange("(g u i e) n -> u g i (e n)", u=2, i=2, e=2)
         w2_raw = stage.tile([P, PACK, N], F32, name="w2_raw", align_bytes=64, offset=W2_RAW_AT)
 
-        nc.sync.dma_start(w1_raw[0][:], w1_rows[:, :, : H // 2])
+        nc.sync.dma_start(w1_raw[0][:], w1_rows[:, 0:2, :])
         nc.sync.dma_start(offsets[:], offs)
         for q in range(4):
             nc.sync.dma_start(scales[32 * q : 32 * q + 4, :].bitcast(I32), x_scales[0, 4 * q : 4 * q + 4, :].bitcast(I32))
-        nc.sync.dma_start(w1_raw[1][:], w1_rows[:, :, H // 2 :])
+        nc.sync.dma_start(w1_raw[1][:], w1_rows[:, 2:4, :])
         nc.sync.dma_start(words[:].bitcast(I32), x_words[0].rearrange("p n t -> p (n t)").bitcast(I32))
         for u in range(2):
             nc.sync.dma_start(w2_raw[:, 2 * u : 2 * u + 2, :].rearrange("p e n -> p (e n)"), w2_rows[u])
@@ -73,9 +73,12 @@ def tile_picked_ypl_loss_p_kernel(tc, x_words, x_scales, w1, w2, in1, in2, offs,
         for half in range(2):
             columns = w1_raw[half][:].rearrange("p j (g u i e) -> p u g j i e", u=2, i=2, e=2)
             for u in (1, 0):
-                dealt = w1_bf[u][:].rearrange("p e (g i j) -> p g j i e", i=2, j=PACK)[:, half * HALF_GROUPS : (half + 1) * HALF_GROUPS]
+                dealt = w1_bf[u][:].rearrange("p e (g i j) -> p g j i e", i=2, j=PACK)[:, :, 2 * half : 2 * half + 2]
                 if half == 1 and u == 1:
                     nc.vector.tensor_copy(dealt, columns[:, u])
+                elif half == 1:
+                    nc.vector.tensor_copy(dealt[:, :HALF_GROUPS], columns[:, u, :HALF_GROUPS])
+                    nc.scalar.copy(dealt[:, HALF_GROUPS:], columns[:, u, HALF_GROUPS:])
                 else:
                     nc.scalar.copy(dealt, columns[:, u])
         x_codes = [stage.tile([P, CHUNK], U32, name=f"x_codes{c}", align_bytes=64, offset=X_CODES_AT[c]) for c in range(CHUNKS)]

@@ -76,7 +76,7 @@ def tile_picked_ypl_loss_p_kernel(tc, x_words, x_scales, w1, w2, in1, in2, offs,
                 dealt = w1_bf[u][:].rearrange("p e (g i j) -> p g j i e", i=2, j=PACK)[:, :, 2 * half : 2 * half + 2]
                 if half == 1 and u == 1:
                     nc.vector.tensor_copy(dealt, columns[:, u])
-                elif half == 1:
+                elif half == 0 and u == 0:
                     nc.vector.tensor_copy(dealt[:, :HALF_GROUPS], columns[:, u, :HALF_GROUPS])
                     nc.scalar.copy(dealt[:, HALF_GROUPS:], columns[:, u, HALF_GROUPS:])
                 else:

@@ -26,16 +26,22 @@ QUERIES = S // D
 OUT_TILES = N // P
 HALF_GROUPS = H // 2 // 8
 LAST = CHUNKS - 1
+GROUPS = H // 8
+SCALAR_GROUPS = ((32, 64), (32, 24))
 EXPONENT_FIELD = 0x7F800000
 LN2 = math.log(2.0)
-VECTOR_CHUNK = 2
+ORDER = (2, 3, 0, 1)
+SLOT = 64
+SIGN_AND_EXPONENT = -(2**23)
+PRODUCT_SHIFT = 64
 
 W1_BF_AT = (0, 2048)
-X_CODES_AT = (W1_BF_AT[1], W1_BF_AT[0], W1_BF_AT[0] + 512, W1_BF_AT[0] + 1024)
 W2_BF_AT = 4096
 W2_RAW_AT = 8192
+X_CODES_AT = (W1_BF_AT[1], W1_BF_AT[0], W1_BF_AT[0] + 512, W1_BF_AT[0] + 1024)
 H_CODES_AT = (W2_RAW_AT, W2_BF_AT + 1024, W2_BF_AT + 2048, W2_BF_AT + 1536)
 W1_CODES_AT = 14336
+WORDS_AT = 16384
 SCALES_AT = W1_CODES_AT - 512
 
 
@@ -51,9 +57,9 @@ def tile_picked_ypl_loss_p_kernel(tc, x_words, x_scales, w1, w2, in1, in2, offs,
         w1_raw = [keep.tile([P, 2, H], F32, name=f"w1_raw{half}", align_bytes=64) for half in range(2)]
         scales = stage.tile([P, T], U8, name="scales", align_bytes=64, offset=SCALES_AT)
         nc.vector.memset(scales[:].bitcast(I32), 0)
-        words = keep.tile([P, T], U32, name="words", align_bytes=64)
+        words = stage.tile([P, T], U32, name="words", align_bytes=64, offset=WORDS_AT)
         w2_rows = w2.rearrange("(g u i e) n -> u g i (e n)", u=2, i=2, e=2)
-        w2_raw = stage.tile([P, PACK, N], F32, name="w2_raw", align_bytes=64, offset=W2_RAW_AT)
+        w2_raw = [stage.tile([P, 2, N], F32, name=f"w2_raw{u}", align_bytes=64, offset=W2_RAW_AT + 2048 * u) for u in range(2)]
 
         nc.sync.dma_start(w1_raw[0][:], w1_rows[:, 0:2, :])
         nc.sync.dma_start(offsets[:], offs)
@@ -62,7 +68,7 @@ def tile_picked_ypl_loss_p_kernel(tc, x_words, x_scales, w1, w2, in1, in2, offs,
         nc.sync.dma_start(w1_raw[1][:], w1_rows[:, 2:4, :])
         nc.sync.dma_start(words[:].bitcast(I32), x_words[0].rearrange("p n t -> p (n t)").bitcast(I32))
         for u in range(2):
-            nc.sync.dma_start(w2_raw[:, 2 * u : 2 * u + 2, :].rearrange("p e n -> p (e n)"), w2_rows[u])
+            nc.sync.dma_start(w2_raw[u][:].rearrange("p e n -> p (e n)"), w2_rows[u])
 
         x_scales_picked = keep.tile([P, S], U8, name="x_scales_picked", align_bytes=64)
         nc.vector.tensor_copy(x_scales_picked[:], scales[:].indirect(offsets[:]))
@@ -74,13 +80,10 @@ def tile_picked_ypl_loss_p_kernel(tc, x_words, x_scales, w1, w2, in1, in2, offs,
             columns = w1_raw[half][:].rearrange("p j (g u i e) -> p u g j i e", u=2, i=2, e=2)
             for u in (1, 0):
                 dealt = w1_bf[u][:].rearrange("p e (g i j) -> p g j i e", i=2, j=PACK)[:, :, 2 * half : 2 * half + 2]
-                if half == 1 and u == 1:
-                    nc.vector.tensor_copy(dealt, columns[:, u])
-                elif half == 0 and u == 0:
-                    nc.vector.tensor_copy(dealt[:, :HALF_GROUPS], columns[:, u, :HALF_GROUPS])
-                    nc.scalar.copy(dealt[:, HALF_GROUPS:], columns[:, u, HALF_GROUPS:])
-                else:
-                    nc.scalar.copy(dealt, columns[:, u])
+                split = SCALAR_GROUPS[half][u]
+                nc.scalar.copy(dealt[:, :split], columns[:, u, :split])
+                if split < GROUPS:
+                    nc.vector.tensor_copy(dealt[:, split:], columns[:, u, split:])
         x_codes = [stage.tile([P, CHUNK], U32, name=f"x_codes{c}", align_bytes=64, offset=X_CODES_AT[c]) for c in range(CHUNKS)]
 
         def quantize_w1(u):
@@ -88,26 +91,34 @@ def tile_picked_ypl_loss_p_kernel(tc, x_words, x_scales, w1, w2, in1, in2, offs,
             nc.vector.quantize_mx(out=w1_codes[:, cols].bitcast(FP8X4), scales=w1_scales[:, cols], in_=w1_bf[u][:].rearrange("p e n -> p (e n)"))
 
         def gather_words(c):
-            nc.vector.tensor_copy(x_codes[c][:], words[:].indirect(offsets[:, c * (CHUNK // 16) : (c + 1) * (CHUNK // 16)]))
+            nc.vector.tensor_copy(x_codes[c][:], words[:].indirect(offsets[:, ORDER[c] * (CHUNK // 16) : (ORDER[c] + 1) * (CHUNK // 16)]))
 
         quantize_w1(1)
         gather_words(0)
         quantize_w1(0)
-        for c in range(1, CHUNKS):
-            gather_words(c)
+        gather_words(1)
+        gather_words(2)
 
-        w2_bf = stage.tile([P, N, PACK], BF16, name="w2_bf", align_bytes=64, offset=W2_BF_AT)
-        nc.vector.tensor_copy(w2_bf[:].rearrange("p (a l) t -> p a t l", l=4), w2_raw[:].rearrange("p t (a l) -> p a t l", l=4))
-        w2_codes = keep.tile([P, N], U32, name="w2_codes", align_bytes=64)
-        w2_scales = keep.tile([P, N], U8, name="w2_scales", align_bytes=64)
-        nc.vector.quantize_mx(out=w2_codes[:].bitcast(FP8X4), scales=w2_scales[:], in_=w2_bf[:].rearrange("p n t -> p (n t)"))
+        w2_bf = [stage.tile([P, N * PACK], BF16, name=f"w2_bf{sign}", align_bytes=64, offset=(W2_BF_AT, WORDS_AT)[sign]) for sign in range(2)]
+        for u, engine_copy in enumerate((nc.scalar.copy, nc.vector.tensor_copy)):
+            engine_copy(
+                w2_bf[0][:].rearrange("p (a l t) -> p a l t", l=4, t=PACK)[:, :, :, 2 * u : 2 * u + 2].rearrange("p a l t -> p a t l"),
+                w2_raw[u][:].rearrange("p t (a l) -> p a t l", l=4),
+            )
+        gather_words(3)
+        nc.vector.tensor_scalar(w2_bf[1][:], w2_bf[0][:], -1.0, None, ALU.mult)
+        w2_codes = keep.tile([P, 2 * N], U32, name="w2_codes", align_bytes=64)
+        w2_scales = keep.tile([P, 2 * N], U8, name="w2_scales", align_bytes=64)
 
-        sums = keep.tile([P, D, OUT_TILES, CHUNKS, CHUNK_QUERIES], F32, name="sums", align_bytes=64)
-        score_sum = keep.tile([P, OUT_TILES, CHUNKS, CHUNK_QUERIES], F32, name="score_sum", align_bytes=64)
+        def quantize_w2(sign):
+            cols = slice(sign * N, (sign + 1) * N)
+            nc.vector.quantize_mx(out=w2_codes[:, cols].bitcast(FP8X4), scales=w2_scales[:, cols], in_=w2_bf[sign][:])
+
+        quantize_w2(0)
 
         h_banks = []
         for c in range(CHUNKS):
-            cols = slice(c * CHUNK, (c + 1) * CHUNK)
+            cols = slice(ORDER[c] * CHUNK, (ORDER[c] + 1) * CHUNK)
             h_bank = psum.tile([P, PACK, CHUNK], F32, name=f"h_bank{c}", tag=f"h_bank{c}")
             for t in (2, 3, 0, 1):
                 nc.tensor.matmul_mx(
@@ -122,83 +133,82 @@ def tile_picked_ypl_loss_p_kernel(tc, x_words, x_scales, w1, w2, in1, in2, offs,
             h_banks.append(h_bank)
 
         h_view = [bank[:].rearrange("p t (v d) -> p d v t", d=D) for bank in h_banks]
-        h_bf = [keep.tile([P, D, CHUNK_QUERIES, PACK], BF16, name=f"h_bf{c}", align_bytes=64) for c in range(CHUNKS - 1)]
-        h_bf.insert(VECTOR_CHUNK, stage.tile([P, D, CHUNK_QUERIES, PACK], BF16, name="h_bf_vector", align_bytes=64, offset=W2_BF_AT))
-        halves = [slice(0, D // 2), slice(D // 2, D)]
-        for c in range(LAST):
-            if c != VECTOR_CHUNK:
-                nc.scalar.activation(h_bf[c][:], h_view[c], ACT.Relu)
-        for part in halves:
-            nc.scalar.activation(h_bf[LAST][:, part], h_view[LAST][:, part], ACT.Relu)
-        h_codes = [stage.tile([P, CHUNK], U32, name=f"h_codes{c}", align_bytes=64, offset=H_CODES_AT[c]) for c in range(CHUNKS)]
+        h_early = keep.tile([P, D, 2, CHUNK_QUERIES, PACK], BF16, name="h_early", align_bytes=64)
+        h_late = keep.tile([P, D, 2, CHUNK_QUERIES, PACK], BF16, name="h_late", align_bytes=64)
+        for c in range(2):
+            nc.scalar.activation(h_early[:, :, c], h_view[c][:, ::-1], ACT.Relu)
+        quantize_w2(1)
+        nc.scalar.activation(h_late[:, :, 0], h_view[2], ACT.Relu)
+        for part in (slice(2, 4), slice(0, 2)):
+            nc.scalar.activation(h_late[:, part, 1], h_view[3][:, part], ACT.Relu)
+        h_codes = keep.tile([P, S], U32, name="h_codes", align_bytes=64)
+        h_scales = keep.tile([P, S], U8, name="h_scales", align_bytes=64)
 
-        def second_product(c, part, bank_tag):
-            cols = slice(part.start * CHUNK_QUERIES, part.stop * CHUNK_QUERIES)
-            width = cols.stop - cols.start
-            h_scales = keep.tile([P, width], U8, name=f"h_scales{c}_{part.start}", align_bytes=64)
-            nc.vector.quantize_mx(out=h_codes[c][:, cols].bitcast(FP8X4), scales=h_scales[:], in_=h_bf[c][:, part].rearrange("p d v t -> p (d v t)"))
-            y_bank = psum.tile([P, OUT_TILES, width], F32, name=f"y_bank{c}_{part.start}", tag=bank_tag)
-            for m in range(OUT_TILES):
-                nc.tensor.matmul_mx(
-                    out=y_bank[:, m, :],
-                    lhsT=w2_codes[:, m * P : (m + 1) * P].bitcast(FP8X4),
-                    lhsT_scale=w2_scales[:, m * P : (m + 1) * P],
-                    rhs=h_codes[c][:, cols].bitcast(FP8X4),
-                    rhs_scale=h_scales[:],
-                    start=True,
-                    stop=True,
-                )
-            scores = y_bank[:].rearrange("p m (d v) -> p m d v", v=CHUNK_QUERIES)
-            nc.scalar.activation(sums[:, part, :, c, :], scores.rearrange("p m d v -> p d m v"), ACT.Exp)
-            return scores
+        def quantize_h(source, first, count, slot):
+            cols = slice(slot * SLOT, (slot + count) * SLOT)
+            nc.vector.quantize_mx(
+                out=h_codes[:, cols].bitcast(FP8X4),
+                scales=h_scales[:, cols],
+                in_=source[:, first : first + count].rearrange("p d c v t -> p (d c v t)"),
+            )
 
-        whole = slice(0, D)
-        chunk_scores = [second_product(0, whole, "y_bank0")]
-        nc.vector.tensor_scalar(h_bf[VECTOR_CHUNK][:], h_view[VECTOR_CHUNK], 0.0, None, ALU.max)
-        chunk_scores.extend([second_product(c, whole, f"y_bank{c}") for c in range(1, LAST)])
-        half_scores = [second_product(LAST, part, tag) for part, tag in zip(halves, (f"y_bank{LAST}", "h_bank0"))]
+        def differences(name, plus, minus, tiles=range(OUT_TILES)):
+            bank = psum.tile([P, len(tiles), 2, SLOT], F32, name=name, tag=name)
+            for m in tiles:
+                for sign, slot in enumerate((plus, minus)):
+                    cols = slice(slot * SLOT, (slot + 2) * SLOT)
+                    stationary = slice(sign * N + m * P, sign * N + (m + 1) * P)
+                    nc.tensor.matmul_mx(
+                        out=bank[:, m - tiles.start].rearrange("p a v -> p (a v)"),
+                        lhsT=w2_codes[:, stationary].bitcast(FP8X4),
+                        lhsT_scale=w2_scales[:, stationary],
+                        rhs=h_codes[:, cols].bitcast(FP8X4),
+                        rhs_scale=h_scales[:, cols],
+                        start=(sign == 0),
+                        stop=(sign == 1),
+                    )
+            return bank[:].rearrange("p m a v -> p a m v")
 
-        def score_sums(c):
-            nc.vector.tensor_reduce(score_sum[:, :, c, :], chunk_scores[c].rearrange("p m d v -> p m v d")[:, :, :, 1:D], mybir.AxisListType.X, ALU.add)
+        q12 = keep.tile([P, 4, OUT_TILES, SLOT], F32, name="q12", align_bytes=64)
+        q3 = keep.tile([P, 2, OUT_TILES, SLOT], F32, name="q3", align_bytes=64)
+        quantize_h(h_early, 2, 2, 4)
+        quantize_h(h_early, 1, 1, 3)
+        quantize_h(h_early, 0, 1, 7)
+        nc.scalar.activation(q12[:, 2:4], differences("early", 4, 3), ACT.Exp)
+        quantize_h(h_late, 2, 1, 2)
+        quantize_h(h_late, 3, 1, 6)
+        nc.scalar.activation(q3[:], differences("third", 2, 6), ACT.Exp)
+        quantize_h(h_late, 0, 2, 0)
+        for m in range(OUT_TILES):
+            nc.scalar.activation(q12[:, 0:2, m : m + 1], differences(f"late{m}", 0, 1, range(m, m + 1)), ACT.Exp)
 
-        places = sums[:].rearrange("p d m c v -> p d m (c v)")
 
-        def add_place(d, queries):
-            nc.vector.tensor_tensor(places[:, d, :, queries], places[:, d - 1, :, queries], places[:, d, :, queries], ALU.add)
+        def wide(name):
+            return keep.tile([P, 2, OUT_TILES * SLOT], F32, name=name, align_bytes=64)
 
-        factor = keep.tile([P, OUT_TILES, QUERIES], F32, name="factor", align_bytes=64)
-        product = keep.tile([P, OUT_TILES, QUERIES], F32, name="product", align_bytes=64)
-        offset = keep.tile([P, OUT_TILES, QUERIES], F32, name="offset", align_bytes=64)
-        early, late = slice(0, QUERIES // 2), slice(QUERIES // 2, QUERIES)
-        add_place(1, early)
-        score_sums(0)
-        add_place(2, early)
-        score_sums(1)
-        add_place(1, late)
-        add_place(3, early)
-        nc.vector.tensor_scalar(factor[:].bitcast(I32), places[:, 1].bitcast(I32), EXPONENT_FIELD, EXPONENT_FIELD, ALU.bitwise_and, ALU.bitwise_xor)
-        add_place(2, late)
-        nc.vector.tensor_tensor(places[:, 0], places[:, 1], factor[:], ALU.mult)
-        add_place(3, late)
-        nc.vector.tensor_tensor(product[:], places[:, 0], places[:, 2], ALU.mult)
-        score_sums(2)
-        upper_scores = keep.tile([P, OUT_TILES, CHUNK_QUERIES], F32, name="upper_scores", align_bytes=64)
-        nc.vector.tensor_reduce(upper_scores[:], half_scores[1].rearrange("p m d v -> p m v d"), mybir.AxisListType.X, ALU.add)
-        nc.vector.tensor_tensor(score_sum[:, :, LAST, :], half_scores[0][:, :, 1, :], upper_scores[:], ALU.add)
-        nc.vector.scalar_tensor_tensor(
-            offset[:], factor[:].bitcast(I32), -LN2 / 2**23, score_sum[:].rearrange("p m c v -> p m (c v)"), ALU.mult, ALU.subtract
+        flat = q12[:].rearrange("p s m v -> p s (m v)")
+        q1, q2 = flat[:, 0:4:3], flat[:, 1:3]
+        second, first, pair, factor, third, product = [wide(name) for name in ("second", "first", "pair", "factor", "third", "product")]
+        steps = (
+            lambda g: nc.vector.scalar_tensor_tensor(second[:, g], q1[:, g], 1.0, q2[:, g], ALU.add, ALU.mult),
+            lambda g: nc.vector.tensor_scalar(first[:, g], q1[:, g], 1.0, 2.0**-PRODUCT_SHIFT, ALU.add, ALU.mult),
+            lambda g: nc.vector.scalar_tensor_tensor(pair[:, g], second[:, g], 1.0, first[:, g], ALU.add, ALU.mult),
+            lambda g: nc.vector.tensor_scalar(
+                factor[:, g].bitcast(I32), pair[:, g].bitcast(I32), EXPONENT_FIELD, SIGN_AND_EXPONENT, ALU.bitwise_and, ALU.bitwise_xor
+            ),
+            lambda g: nc.vector.tensor_tensor(first[:, g], pair[:, g], factor[:, g], ALU.mult),
         )
-
-        partial = []
+        late, early = 0, 1
+        q3_flat = q3[:].rearrange("p g m v -> p g (m v)")
+        for g in (early, late):
+            for step in steps[:3]:
+                step(g)
+            nc.vector.scalar_tensor_tensor(third[:, g], second[:, g], 1.0, q3_flat[:, g], ALU.add, ALU.mult)
+            nc.vector.scalar_tensor_tensor(product[:, g], third[:, g], 1.0, pair[:, g], ALU.add, ALU.mult)
         for m in range(OUT_TILES):
-            log_last = keep.tile([P, QUERIES], F32, name=f"log_last{m}", align_bytes=64)
-            nc.scalar.activation(log_last[:], places[:, 3, m, :], ACT.Ln)
-            rest = keep.tile([P, QUERIES], F32, name=f"rest{m}", align_bytes=64)
-            nc.vector.scalar_tensor_tensor(rest[:], log_last[:], 128 * LN2, offset[:, m], ALU.add, ALU.add)
-            partial.append(rest)
-        for m in range(OUT_TILES):
-            log_product = keep.tile([P, QUERIES], F32, name=f"log_product{m}", align_bytes=64)
-            nc.scalar.activation(log_product[:], product[:, m], ACT.Ln, scale=0.5)
-            result = keep.tile([P, QUERIES], F32, name=f"result{m}", align_bytes=64)
-            nc.vector.tensor_tensor(result[:], log_product[:], partial[m][:], ALU.add)
-            nc.sync.dma_start(out[m * P : (m + 1) * P, :], result[:])
+            cols = slice(m * SLOT, (m + 1) * SLOT)
+            log_product = keep.tile([P, 2, SLOT], F32, name=f"log_product{m}", align_bytes=64)
+            nc.scalar.activation(log_product[:], product[:, :, cols], ACT.Ln)
+            result = keep.tile([P, 2, SLOT], F32, name=f"result{m}", align_bytes=64)
+            nc.vector.tensor_scalar(result[:], log_product[:], PRODUCT_SHIFT * LN2, None, ALU.add)
+            nc.sync.dma_start(out[m * P : (m + 1) * P, :], result[:].rearrange("p g v -> p (g v)"))

@@ -30,7 +30,7 @@ GROUPS = H // 8
 SCALAR_GROUPS = ((32, 64), (32, 24))
 EXPONENT_FIELD = 0x7F800000
 LN2 = math.log(2.0)
-ORDER = (2, 3, 0, 1)
+ORDER = (2, 3, 1, 0)
 SLOT = 64
 SIGN_AND_EXPONENT = -(2**23)
 PRODUCT_SHIFT = 64
@@ -42,7 +42,7 @@ X_CODES_AT = (W1_BF_AT[1], W1_BF_AT[0], W1_BF_AT[0] + 512, W1_BF_AT[0] + 1024)
 H_CODES_AT = (W2_RAW_AT, W2_BF_AT + 1024, W2_BF_AT + 2048, W2_BF_AT + 1536)
 W1_CODES_AT = 14336
 WORDS_AT = 16384
-SCALES_AT = W1_CODES_AT - 512
+SCALES_AT = 20480
 
 
 def tile_picked_ypl_loss_p_kernel(tc, x_words, x_scales, w1, w2, in1, in2, offs, out):
@@ -63,15 +63,15 @@ def tile_picked_ypl_loss_p_kernel(tc, x_words, x_scales, w1, w2, in1, in2, offs,
 
         nc.sync.dma_start(w1_raw[0][:], w1_rows[:, 0:2, :])
         nc.sync.dma_start(offsets[:], offs)
-        for q in range(4):
+        for q in (0, 2, 1, 3):
             nc.sync.dma_start(scales[32 * q : 32 * q + 4, :].bitcast(I32), x_scales[0, 4 * q : 4 * q + 4, :].bitcast(I32))
         nc.sync.dma_start(w1_raw[1][:], w1_rows[:, 2:4, :])
         nc.sync.dma_start(words[:].bitcast(I32), x_words[0].rearrange("p n t -> p (n t)").bitcast(I32))
         for u in range(2):
             nc.sync.dma_start(w2_raw[u][:].rearrange("p e n -> p (e n)"), w2_rows[u])
 
-        x_scales_picked = keep.tile([P, S], U8, name="x_scales_picked", align_bytes=64)
-        nc.vector.tensor_copy(x_scales_picked[:], scales[:].indirect(offsets[:]))
+        x_scales_picked = keep.tile([P, S - CHUNK], U8, name="x_scales_picked", align_bytes=64)
+        nc.vector.tensor_copy(x_scales_picked[:], scales[:].indirect(offsets[:, CHUNK // 16 :]))
 
         w1_codes = stage.tile([P, H], U32, name="w1_codes", align_bytes=64, offset=W1_CODES_AT)
         w1_scales = keep.tile([P, H], U8, name="w1_scales", align_bytes=64)
@@ -84,28 +84,31 @@ def tile_picked_ypl_loss_p_kernel(tc, x_words, x_scales, w1, w2, in1, in2, offs,
                 nc.scalar.copy(dealt[:, :split], columns[:, u, :split])
                 if split < GROUPS:
                     nc.vector.tensor_copy(dealt[:, split:], columns[:, u, split:])
-        x_codes = [stage.tile([P, CHUNK], U32, name=f"x_codes{c}", align_bytes=64, offset=X_CODES_AT[c]) for c in range(CHUNKS)]
+        x_early = [stage.tile([P, CHUNK], U32, name=f"x_codes{c}", align_bytes=64, offset=X_CODES_AT[c]) for c in range(2)]
+        x_late = stage.tile([P, 2 * CHUNK], U32, name="x_late", align_bytes=64, offset=X_CODES_AT[2])
+        x_codes = [x_early[0][:], x_early[1][:], x_late[:, CHUNK : 2 * CHUNK], x_late[:, 0:CHUNK]]
 
         def quantize_w1(u):
             cols = slice(2 * u * P, 2 * (u + 1) * P)
             nc.vector.quantize_mx(out=w1_codes[:, cols].bitcast(FP8X4), scales=w1_scales[:, cols], in_=w1_bf[u][:].rearrange("p e n -> p (e n)"))
 
         def gather_words(c):
-            nc.vector.tensor_copy(x_codes[c][:], words[:].indirect(offsets[:, ORDER[c] * (CHUNK // 16) : (ORDER[c] + 1) * (CHUNK // 16)]))
+            nc.vector.tensor_copy(x_codes[c], words[:].indirect(offsets[:, ORDER[c] * (CHUNK // 16) : (ORDER[c] + 1) * (CHUNK // 16)]))
 
         quantize_w1(1)
         gather_words(0)
         quantize_w1(0)
         gather_words(1)
-        gather_words(2)
+        nc.vector.tensor_copy(x_late[:], words[:].indirect(offsets[:, 0 : 2 * CHUNK // 16]))
 
-        w2_bf = [stage.tile([P, N * PACK], BF16, name=f"w2_bf{sign}", align_bytes=64, offset=(W2_BF_AT, WORDS_AT)[sign]) for sign in range(2)]
+        w2_bf = [stage.tile([P, N * PACK], BF16, name=f"w2_bf{sign}", align_bytes=64, offset=(W2_BF_AT, SCALES_AT)[sign]) for sign in range(2)]
         for u, engine_copy in enumerate((nc.scalar.copy, nc.vector.tensor_copy)):
             engine_copy(
                 w2_bf[0][:].rearrange("p (a l t) -> p a l t", l=4, t=PACK)[:, :, :, 2 * u : 2 * u + 2].rearrange("p a l t -> p a t l"),
                 w2_raw[u][:].rearrange("p t (a l) -> p a t l", l=4),
             )
-        gather_words(3)
+        x_scales_last = stage.tile([P, CHUNK], U8, name="x_scales_last", align_bytes=64, offset=W2_RAW_AT + 2048)
+        nc.vector.tensor_copy(x_scales_last[:], scales[:].indirect(offsets[:, 0 : CHUNK // 16]))
         nc.vector.tensor_scalar(w2_bf[1][:], w2_bf[0][:], -1.0, None, ALU.mult)
         w2_codes = keep.tile([P, 2 * N], U32, name="w2_codes", align_bytes=64)
         w2_scales = keep.tile([P, 2 * N], U8, name="w2_scales", align_bytes=64)
@@ -118,15 +121,15 @@ def tile_picked_ypl_loss_p_kernel(tc, x_words, x_scales, w1, w2, in1, in2, offs,
 
         h_banks = []
         for c in range(CHUNKS):
-            cols = slice(ORDER[c] * CHUNK, (ORDER[c] + 1) * CHUNK)
+            plane = x_scales_last[:] if c == LAST else x_scales_picked[:, (ORDER[c] - 1) * CHUNK : ORDER[c] * CHUNK]
             h_bank = psum.tile([P, PACK, CHUNK], F32, name=f"h_bank{c}", tag=f"h_bank{c}")
             for t in (2, 3, 0, 1):
                 nc.tensor.matmul_mx(
                     out=h_bank[:, t, :],
                     lhsT=w1_codes[:, t * P : (t + 1) * P].bitcast(FP8X4),
                     lhsT_scale=w1_scales[:, t * P : (t + 1) * P],
-                    rhs=x_codes[c][:].bitcast(FP8X4),
-                    rhs_scale=x_scales_picked[:, cols],
+                    rhs=x_codes[c].bitcast(FP8X4),
+                    rhs_scale=plane,
                     start=True,
                     stop=True,
                 )
@@ -138,9 +141,9 @@ def tile_picked_ypl_loss_p_kernel(tc, x_words, x_scales, w1, w2, in1, in2, offs,
         for c in range(2):
             nc.scalar.activation(h_early[:, :, c], h_view[c][:, ::-1], ACT.Relu)
         quantize_w2(1)
-        nc.scalar.activation(h_late[:, :, 0], h_view[2], ACT.Relu)
+        nc.scalar.activation(h_late[:, :, 1], h_view[2], ACT.Relu)
         for part in (slice(2, 4), slice(0, 2)):
-            nc.scalar.activation(h_late[:, part, 1], h_view[3][:, part], ACT.Relu)
+            nc.scalar.activation(h_late[:, part, 0], h_view[3][:, part], ACT.Relu)
         h_codes = keep.tile([P, S], U32, name="h_codes", align_bytes=64)
         h_scales = keep.tile([P, S], U8, name="h_scales", align_bytes=64)
 

@@ -22,27 +22,21 @@ PACK = 4
 CHUNK = 128
 CHUNKS = S // CHUNK
 CHUNK_QUERIES = CHUNK // D
-QUERIES = S // D
 OUT_TILES = N // P
-HALF_GROUPS = H // 2 // 8
 LAST = CHUNKS - 1
 GROUPS = H // 8
 SCALAR_GROUPS = ((32, 64), (32, 24))
-EXPONENT_FIELD = 0x7F800000
-LN2 = math.log(2.0)
 ORDER = (2, 3, 1, 0)
 SLOT = 64
-SIGN_AND_EXPONENT = -(2**23)
 PRODUCT_SHIFT = 64
+LN2 = math.log(2.0)
 
 W1_BF_AT = (0, 2048)
-W2_BF_AT = 4096
-W2_RAW_AT = 8192
-X_CODES_AT = (W1_BF_AT[1], W1_BF_AT[0], W1_BF_AT[0] + 512, W1_BF_AT[0] + 1024)
-H_CODES_AT = (W2_RAW_AT, W2_BF_AT + 1024, W2_BF_AT + 2048, W2_BF_AT + 1536)
-W1_CODES_AT = 14336
-WORDS_AT = 16384
-SCALES_AT = 20480
+WORDS_AT = 4096
+SCALES_AT = 8192
+W2_RAW_AT = (10240, 12288)
+X_CODES_AT = (W1_BF_AT[1], W1_BF_AT[1] + 512, W1_BF_AT[1] + 1024)
+X_SCALES_LAST_AT = W2_RAW_AT[0]
 
 
 def tile_picked_ypl_loss_p_kernel(tc, x_words, x_scales, w1, w2, in1, in2, offs, out):
@@ -59,7 +53,7 @@ def tile_picked_ypl_loss_p_kernel(tc, x_words, x_scales, w1, w2, in1, in2, offs,
         nc.vector.memset(scales[:].bitcast(I32), 0)
         words = stage.tile([P, T], U32, name="words", align_bytes=64, offset=WORDS_AT)
         w2_rows = w2.rearrange("(g u i e) n -> u g i (e n)", u=2, i=2, e=2)
-        w2_raw = [stage.tile([P, 2, N], F32, name=f"w2_raw{u}", align_bytes=64, offset=W2_RAW_AT + 2048 * u) for u in range(2)]
+        w2_raw = [stage.tile([P, 2, N], F32, name=f"w2_raw{u}", align_bytes=64, offset=W2_RAW_AT[u]) for u in range(2)]
 
         nc.sync.dma_start(w1_raw[0][:], w1_rows[:, 0:2, :])
         nc.sync.dma_start(offsets[:], offs)
@@ -70,10 +64,10 @@ def tile_picked_ypl_loss_p_kernel(tc, x_words, x_scales, w1, w2, in1, in2, offs,
         for u in range(2):
             nc.sync.dma_start(w2_raw[u][:].rearrange("p e n -> p (e n)"), w2_rows[u])
 
-        x_scales_picked = keep.tile([P, S - CHUNK], U8, name="x_scales_picked", align_bytes=64)
-        nc.vector.tensor_copy(x_scales_picked[:], scales[:].indirect(offsets[:, CHUNK // 16 :]))
+        x_scales_early = keep.tile([P, S - CHUNK], U8, name="x_scales_early", align_bytes=64)
+        nc.vector.tensor_copy(x_scales_early[:], scales[:].indirect(offsets[:, CHUNK // 16 :]))
 
-        w1_codes = stage.tile([P, H], U32, name="w1_codes", align_bytes=64, offset=W1_CODES_AT)
+        w1_codes = keep.tile([P, H], U32, name="w1_codes", align_bytes=64)
         w1_scales = keep.tile([P, H], U8, name="w1_scales", align_bytes=64)
         w1_bf = [stage.tile([P, 2, P * PACK], BF16, name=f"w1_bf{u}", align_bytes=64, offset=W1_BF_AT[u]) for u in range(2)]
         for half in range(2):
@@ -87,6 +81,8 @@ def tile_picked_ypl_loss_p_kernel(tc, x_words, x_scales, w1, w2, in1, in2, offs,
         x_early = [stage.tile([P, CHUNK], U32, name=f"x_codes{c}", align_bytes=64, offset=X_CODES_AT[c]) for c in range(2)]
         x_late = stage.tile([P, 2 * CHUNK], U32, name="x_late", align_bytes=64, offset=X_CODES_AT[2])
         x_codes = [x_early[0][:], x_early[1][:], x_late[:, CHUNK : 2 * CHUNK], x_late[:, 0:CHUNK]]
+        x_scales_last = stage.tile([P, CHUNK], U8, name="x_scales_last", align_bytes=64, offset=X_SCALES_LAST_AT)
+        planes = [x_scales_early[:, (ORDER[c] - 1) * CHUNK : ORDER[c] * CHUNK] for c in range(LAST)] + [x_scales_last[:]]
 
         def quantize_w1(u):
             cols = slice(2 * u * P, 2 * (u + 1) * P)
@@ -95,20 +91,44 @@ def tile_picked_ypl_loss_p_kernel(tc, x_words, x_scales, w1, w2, in1, in2, offs,
         def gather_words(c):
             nc.vector.tensor_copy(x_codes[c], words[:].indirect(offsets[:, ORDER[c] * (CHUNK // 16) : (ORDER[c] + 1) * (CHUNK // 16)]))
 
+        def gather_scales(c):
+            nc.vector.tensor_copy(planes[c], scales[:].indirect(offsets[:, ORDER[c] * (CHUNK // 16) : (ORDER[c] + 1) * (CHUNK // 16)]))
+
         quantize_w1(1)
-        gather_words(0)
         quantize_w1(0)
-        gather_words(1)
+        for c in range(2):
+            gather_words(c)
         nc.vector.tensor_copy(x_late[:], words[:].indirect(offsets[:, 0 : 2 * CHUNK // 16]))
 
-        w2_bf = [stage.tile([P, N * PACK], BF16, name=f"w2_bf{sign}", align_bytes=64, offset=(W2_BF_AT, SCALES_AT)[sign]) for sign in range(2)]
-        for u, engine_copy in enumerate((nc.scalar.copy, nc.vector.tensor_copy)):
-            engine_copy(
-                w2_bf[0][:].rearrange("p (a l t) -> p a l t", l=4, t=PACK)[:, :, :, 2 * u : 2 * u + 2].rearrange("p a l t -> p a t l"),
-                w2_raw[u][:].rearrange("p t (a l) -> p a t l", l=4),
-            )
-        x_scales_last = stage.tile([P, CHUNK], U8, name="x_scales_last", align_bytes=64, offset=W2_RAW_AT + 2048)
-        nc.vector.tensor_copy(x_scales_last[:], scales[:].indirect(offsets[:, 0 : CHUNK // 16]))
+        h_banks = [psum.tile([P, PACK, CHUNK], F32, name=f"h_bank{c}", tag=f"h_bank{c}") for c in range(CHUNKS)]
+
+        def first_product(c):
+            for t in (2, 3, 0, 1):
+                nc.tensor.matmul_mx(
+                    out=h_banks[c][:, t, :],
+                    lhsT=w1_codes[:, t * P : (t + 1) * P].bitcast(FP8X4),
+                    lhsT_scale=w1_scales[:, t * P : (t + 1) * P],
+                    rhs=x_codes[c].bitcast(FP8X4),
+                    rhs_scale=planes[c],
+                    start=True,
+                    stop=True,
+                )
+
+        for c in range(2):
+            first_product(c)
+
+        w2_bf = [
+            keep.tile([P, N * PACK], BF16, name="w2_bf", align_bytes=64),
+            keep.tile([P, N * PACK], BF16, name="w2_neg", align_bytes=64),
+        ]
+
+        def w2_views(u):
+            dealt = w2_bf[0][:].rearrange("p (a l t) -> p a l t", l=4, t=PACK)[:, :, :, 2 * u : 2 * u + 2].rearrange("p a l t -> p a t l")
+            return dealt, w2_raw[u][:].rearrange("p t (a l) -> p a t l", l=4)
+
+        nc.scalar.copy(*w2_views(0))
+        nc.vector.tensor_copy(*w2_views(1))
+        gather_scales(LAST)
         nc.vector.tensor_scalar(w2_bf[1][:], w2_bf[0][:], -1.0, None, ALU.mult)
         w2_codes = keep.tile([P, 2 * N], U32, name="w2_codes", align_bytes=64)
         w2_scales = keep.tile([P, 2 * N], U8, name="w2_scales", align_bytes=64)
@@ -117,33 +137,18 @@ def tile_picked_ypl_loss_p_kernel(tc, x_words, x_scales, w1, w2, in1, in2, offs,
             cols = slice(sign * N, (sign + 1) * N)
             nc.vector.quantize_mx(out=w2_codes[:, cols].bitcast(FP8X4), scales=w2_scales[:, cols], in_=w2_bf[sign][:])
 
-        quantize_w2(0)
-
-        h_banks = []
-        for c in range(CHUNKS):
-            plane = x_scales_last[:] if c == LAST else x_scales_picked[:, (ORDER[c] - 1) * CHUNK : ORDER[c] * CHUNK]
-            h_bank = psum.tile([P, PACK, CHUNK], F32, name=f"h_bank{c}", tag=f"h_bank{c}")
-            for t in (2, 3, 0, 1):
-                nc.tensor.matmul_mx(
-                    out=h_bank[:, t, :],
-                    lhsT=w1_codes[:, t * P : (t + 1) * P].bitcast(FP8X4),
-                    lhsT_scale=w1_scales[:, t * P : (t + 1) * P],
-                    rhs=x_codes[c].bitcast(FP8X4),
-                    rhs_scale=plane,
-                    start=True,
-                    stop=True,
-                )
-            h_banks.append(h_bank)
+        for c in range(2, CHUNKS):
+            first_product(c)
 
         h_view = [bank[:].rearrange("p t (v d) -> p d v t", d=D) for bank in h_banks]
         h_early = keep.tile([P, D, 2, CHUNK_QUERIES, PACK], BF16, name="h_early", align_bytes=64)
         h_late = keep.tile([P, D, 2, CHUNK_QUERIES, PACK], BF16, name="h_late", align_bytes=64)
         for c in range(2):
             nc.scalar.activation(h_early[:, :, c], h_view[c][:, ::-1], ACT.Relu)
+        quantize_w2(0)
         quantize_w2(1)
-        nc.scalar.activation(h_late[:, :, 1], h_view[2], ACT.Relu)
-        for part in (slice(2, 4), slice(0, 2)):
-            nc.scalar.activation(h_late[:, part, 0], h_view[3][:, part], ACT.Relu)
+        for c, part in ((2, slice(0, 4)), (3, slice(2, 4)), (3, slice(0, 2))):
+            nc.scalar.activation(h_late[:, part, LAST - c], h_view[c][:, part], ACT.Relu)
         h_codes = keep.tile([P, S], U32, name="h_codes", align_bytes=64)
         h_scales = keep.tile([P, S], U8, name="h_scales", align_bytes=64)
 
@@ -155,21 +160,24 @@ def tile_picked_ypl_loss_p_kernel(tc, x_words, x_scales, w1, w2, in1, in2, offs,
                 in_=source[:, first : first + count].rearrange("p d c v t -> p (d c v t)"),
             )
 
-        def differences(name, plus, minus, tiles=range(OUT_TILES)):
-            bank = psum.tile([P, len(tiles), 2, SLOT], F32, name=name, tag=name)
-            for m in tiles:
+        def score_pass(target, m, sign, slot, start):
+            cols = slice(slot * SLOT, (slot + 2) * SLOT)
+            stationary = slice(sign * N + m * P, sign * N + (m + 1) * P)
+            nc.tensor.matmul_mx(
+                out=target,
+                lhsT=w2_codes[:, stationary].bitcast(FP8X4),
+                lhsT_scale=w2_scales[:, stationary],
+                rhs=h_codes[:, cols].bitcast(FP8X4),
+                rhs_scale=h_scales[:, cols],
+                start=start,
+                stop=not start,
+            )
+
+        def differences(name, plus, minus):
+            bank = psum.tile([P, OUT_TILES, 2, SLOT], F32, name=name, tag=name)
+            for m in range(OUT_TILES):
                 for sign, slot in enumerate((plus, minus)):
-                    cols = slice(slot * SLOT, (slot + 2) * SLOT)
-                    stationary = slice(sign * N + m * P, sign * N + (m + 1) * P)
-                    nc.tensor.matmul_mx(
-                        out=bank[:, m - tiles.start].rearrange("p a v -> p (a v)"),
-                        lhsT=w2_codes[:, stationary].bitcast(FP8X4),
-                        lhsT_scale=w2_scales[:, stationary],
-                        rhs=h_codes[:, cols].bitcast(FP8X4),
-                        rhs_scale=h_scales[:, cols],
-                        start=(sign == 0),
-                        stop=(sign == 1),
-                    )
+                    score_pass(bank[:, m].rearrange("p a v -> p (a v)"), m, sign, slot, sign == 0)
             return bank[:].rearrange("p m a v -> p a m v")
 
         q12 = keep.tile([P, 4, OUT_TILES, SLOT], F32, name="q12", align_bytes=64)
@@ -181,31 +189,25 @@ def tile_picked_ypl_loss_p_kernel(tc, x_words, x_scales, w1, w2, in1, in2, offs,
         quantize_h(h_late, 2, 1, 2)
         quantize_h(h_late, 3, 1, 6)
         nc.scalar.activation(q3[:], differences("third", 2, 6), ACT.Exp)
+        late_banks = [psum.tile([P, 2, SLOT], F32, name=f"late{m}", tag=f"late{m}") for m in range(OUT_TILES)]
         quantize_h(h_late, 0, 2, 0)
         for m in range(OUT_TILES):
-            nc.scalar.activation(q12[:, 0:2, m : m + 1], differences(f"late{m}", 0, 1, range(m, m + 1)), ACT.Exp)
-
+            for sign in range(2):
+                score_pass(late_banks[m][:].rearrange("p a v -> p (a v)"), m, sign, sign, sign == 0)
+            nc.scalar.activation(q12[:, 0:2, m], late_banks[m][:], ACT.Exp)
 
         def wide(name):
             return keep.tile([P, 2, OUT_TILES * SLOT], F32, name=name, align_bytes=64)
 
         flat = q12[:].rearrange("p s m v -> p s (m v)")
         q1, q2 = flat[:, 0:4:3], flat[:, 1:3]
-        second, first, pair, factor, third, product = [wide(name) for name in ("second", "first", "pair", "factor", "third", "product")]
-        steps = (
-            lambda g: nc.vector.scalar_tensor_tensor(second[:, g], q1[:, g], 1.0, q2[:, g], ALU.add, ALU.mult),
-            lambda g: nc.vector.tensor_scalar(first[:, g], q1[:, g], 1.0, 2.0**-PRODUCT_SHIFT, ALU.add, ALU.mult),
-            lambda g: nc.vector.scalar_tensor_tensor(pair[:, g], second[:, g], 1.0, first[:, g], ALU.add, ALU.mult),
-            lambda g: nc.vector.tensor_scalar(
-                factor[:, g].bitcast(I32), pair[:, g].bitcast(I32), EXPONENT_FIELD, SIGN_AND_EXPONENT, ALU.bitwise_and, ALU.bitwise_xor
-            ),
-            lambda g: nc.vector.tensor_tensor(first[:, g], pair[:, g], factor[:, g], ALU.mult),
-        )
+        second, first, pair, third, product = [wide(name) for name in ("second", "first", "pair", "third", "product")]
         late, early = 0, 1
         q3_flat = q3[:].rearrange("p g m v -> p g (m v)")
         for g in (early, late):
-            for step in steps[:3]:
-                step(g)
+            nc.vector.scalar_tensor_tensor(second[:, g], q1[:, g], 1.0, q2[:, g], ALU.add, ALU.mult)
+            nc.vector.tensor_scalar(first[:, g], q1[:, g], 1.0, 2.0**-PRODUCT_SHIFT, ALU.add, ALU.mult)
+            nc.vector.scalar_tensor_tensor(pair[:, g], second[:, g], 1.0, first[:, g], ALU.add, ALU.mult)
             nc.vector.scalar_tensor_tensor(third[:, g], second[:, g], 1.0, q3_flat[:, g], ALU.add, ALU.mult)
             nc.vector.scalar_tensor_tensor(product[:, g], third[:, g], 1.0, pair[:, g], ALU.add, ALU.mult)
         for m in range(OUT_TILES):

@@ -201,15 +201,21 @@ def tile_picked_ypl_loss_p_kernel(tc, x_words, x_scales, w1, w2, in1, in2, offs,
 
         flat = q12[:].rearrange("p s m v -> p s (m v)")
         q1, q2 = flat[:, 0:4:3], flat[:, 1:3]
+        q3_flat = q3[:].rearrange("p g m v -> p g (m v)")
         second, first, pair, third, product = [wide(name) for name in ("second", "first", "pair", "third", "product")]
         late, early = 0, 1
-        q3_flat = q3[:].rearrange("p g m v -> p g (m v)")
+
+        def plus_one_times(target, left, right):
+            nc.vector.scalar_tensor_tensor(target, left, 1.0, right, ALU.add, ALU.mult)
+
         for g in (early, late):
-            nc.vector.scalar_tensor_tensor(second[:, g], q1[:, g], 1.0, q2[:, g], ALU.add, ALU.mult)
+            plus_one_times(second[:, g], q1[:, g], q2[:, g])
             nc.vector.tensor_scalar(first[:, g], q1[:, g], 1.0, 2.0**-PRODUCT_SHIFT, ALU.add, ALU.mult)
-            nc.vector.scalar_tensor_tensor(pair[:, g], second[:, g], 1.0, first[:, g], ALU.add, ALU.mult)
-            nc.vector.scalar_tensor_tensor(third[:, g], second[:, g], 1.0, q3_flat[:, g], ALU.add, ALU.mult)
-            nc.vector.scalar_tensor_tensor(product[:, g], third[:, g], 1.0, pair[:, g], ALU.add, ALU.mult)
+            plus_one_times(third[:, g], second[:, g], q3_flat[:, g])
+            plus_one_times(pair[:, g], second[:, g], first[:, g])
+        for m in range(OUT_TILES):
+            cols = slice(m * SLOT, (m + 1) * SLOT)
+            plus_one_times(product[:, :, cols], third[:, :, cols], pair[:, :, cols])
         for m in range(OUT_TILES):
             cols = slice(m * SLOT, (m + 1) * SLOT)
             log_product = keep.tile([P, 2, SLOT], F32, name=f"log_product{m}", align_bytes=64)

@@ -25,7 +25,7 @@ CHUNK_QUERIES = CHUNK // D
 OUT_TILES = N // P
 LAST = CHUNKS - 1
 GROUPS = H // 8
-SCALAR_GROUPS = ((32, 64), (32, 24))
+SCALAR_GROUPS = ((32, 64), (24, 24))
 ORDER = (2, 3, 1, 0)
 SLOT = 64
 PRODUCT_SHIFT = 64
@@ -160,7 +160,7 @@ def tile_picked_ypl_loss_p_kernel(tc, x_words, x_scales, w1, w2, in1, in2, offs,
                 in_=source[:, first : first + count].rearrange("p d c v t -> p (d c v t)"),
             )
 
-        def score_pass(target, m, sign, slot, start):
+        def score_pass(target, m, sign, slot, start, stop):
             cols = slice(slot * SLOT, (slot + 2) * SLOT)
             stationary = slice(sign * N + m * P, sign * N + (m + 1) * P)
             nc.tensor.matmul_mx(
@@ -170,14 +170,14 @@ def tile_picked_ypl_loss_p_kernel(tc, x_words, x_scales, w1, w2, in1, in2, offs,
                 rhs=h_codes[:, cols].bitcast(FP8X4),
                 rhs_scale=h_scales[:, cols],
                 start=start,
-                stop=not start,
+                stop=stop,
             )
 
         def differences(name, plus, minus):
             bank = psum.tile([P, OUT_TILES, 2, SLOT], F32, name=name, tag=name)
-            for m in range(OUT_TILES):
-                for sign, slot in enumerate((plus, minus)):
-                    score_pass(bank[:, m].rearrange("p a v -> p (a v)"), m, sign, slot, sign == 0)
+            for sign, slot in enumerate((plus, minus)):
+                for m in range(OUT_TILES):
+                    score_pass(bank[:, m].rearrange("p a v -> p (a v)"), m, sign, slot, (sign, m) == (0, 0), (sign, m) == (1, OUT_TILES - 1))
             return bank[:].rearrange("p m a v -> p a m v")
 
         q12 = keep.tile([P, 4, OUT_TILES, SLOT], F32, name="q12", align_bytes=64)
@@ -193,7 +193,7 @@ def tile_picked_ypl_loss_p_kernel(tc, x_words, x_scales, w1, w2, in1, in2, offs,
         quantize_h(h_late, 0, 2, 0)
         for m in range(OUT_TILES):
             for sign in range(2):
-                score_pass(late_banks[m][:].rearrange("p a v -> p (a v)"), m, sign, sign, sign == 0)
+                score_pass(late_banks[m][:].rearrange("p a v -> p (a v)"), m, sign, sign, sign == 0, sign == 1)
             nc.scalar.activation(q12[:, 0:2, m], late_banks[m][:], ACT.Exp)
 
         def wide(name):

@@ -141,13 +141,13 @@ def tile_picked_ypl_loss_p_kernel(tc, x_words, x_scales, w1, w2, in1, in2, offs,
             first_product(c)
 
         h_view = [bank[:].rearrange("p t (v d) -> p d v t", d=D) for bank in h_banks]
-        h_early = keep.tile([P, D, 2, CHUNK_QUERIES, PACK], BF16, name="h_early", align_bytes=64)
-        h_late = keep.tile([P, D, 2, CHUNK_QUERIES, PACK], BF16, name="h_late", align_bytes=64)
+        h_bf = keep.tile([P, 2 * D, 2, CHUNK_QUERIES, PACK], BF16, name="h_bf", align_bytes=64)
+        h_late, h_early = h_bf[:, :D], h_bf[:, D:]
         for c in range(2):
             nc.scalar.activation(h_early[:, :, c], h_view[c][:, ::-1], ACT.Relu)
         quantize_w2(0)
         quantize_w2(1)
-        for c, part in ((2, slice(0, 4)), (3, slice(2, 4)), (3, slice(0, 2))):
+        for c, part in ((2, slice(0, 3)), (3, slice(2, 4)), (3, slice(0, 2))):
             nc.scalar.activation(h_late[:, part, LAST - c], h_view[c][:, part], ACT.Relu)
         h_codes = keep.tile([P, S], U32, name="h_codes", align_bytes=64)
         h_scales = keep.tile([P, S], U8, name="h_scales", align_bytes=64)
@@ -184,10 +184,10 @@ def tile_picked_ypl_loss_p_kernel(tc, x_words, x_scales, w1, w2, in1, in2, offs,
         q3 = keep.tile([P, 2, OUT_TILES, SLOT], F32, name="q3", align_bytes=64)
         quantize_h(h_early, 2, 2, 4)
         quantize_h(h_early, 1, 1, 3)
-        quantize_h(h_early, 0, 1, 7)
+        nc.vector.tensor_scalar(h_late[:, 3, 1], h_view[2][:, 3], 0.0, None, ALU.max)
         nc.scalar.activation(q12[:, 2:4], differences("early", 4, 3), ACT.Exp)
         quantize_h(h_late, 2, 1, 2)
-        quantize_h(h_late, 3, 1, 6)
+        quantize_h(h_bf, 3, 2, 6)
         nc.scalar.activation(q3[:], differences("third", 2, 6), ACT.Exp)
         late_banks = [psum.tile([P, 2, SLOT], F32, name=f"late{m}", tag=f"late{m}") for m in range(OUT_TILES)]
         quantize_h(h_late, 0, 2, 0)

import math
from contextlib import ExitStack

import concourse.mybir as mybir

K, T, S, D, H, N = 512, 1024, 512, 4, 512, 256
FLOPS = 2 * K * H * S + 2 * H * N * S
BYTES = K * T + (K // 32) * T + 4 * K * H + 4 * H * N + 2 * 128 * (S // 16) + 4 * N * (S // D)

F32 = mybir.dt.float32
BF16 = mybir.dt.bfloat16
I32 = mybir.dt.int32
U32 = mybir.dt.uint32
U16 = mybir.dt.uint16
U8 = mybir.dt.uint8
FP8X4 = mybir.dt.float8_e4m3fn_x4
ACT = mybir.ActivationFunctionType
ALU = mybir.AluOpType

P = 128
PACK = 4
CHUNK = 128
CHUNKS = S // CHUNK
CHUNK_QUERIES = CHUNK // D
OUT_TILES = N // P
LAST = CHUNKS - 1
GROUPS = H // 8
SCALAR_GROUPS = ((32, 64), (24, 24))
ORDER = (2, 3, 1, 0)
SLOT = 64
PRODUCT_SHIFT = 64
LN2 = math.log(2.0)

W1_BF_AT = (0, 2048)
WORDS_AT = 4096
SCALES_AT = 8192
W2_RAW_AT = (10240, 12288)
X_CODES_AT = (W1_BF_AT[1], W1_BF_AT[1] + 512, W1_BF_AT[1] + 1024)
X_SCALES_LAST_AT = W2_RAW_AT[0]


def tile_picked_ypl_loss_p_kernel(tc, x_words, x_scales, w1, w2, in1, in2, offs, out):
    nc = tc.nc
    with ExitStack() as ctx:
        keep = ctx.enter_context(tc.tile_pool(name="keep", bufs=1))
        stage = ctx.enter_context(tc.tile_pool(name="stage", bufs=1))
        psum = ctx.enter_context(tc.psum_pool(name="psum", bufs=1))

        offsets = keep.tile([P, S // 16], U16, name="offsets")
        w1_rows = w1.rearrange("(p j) c -> p j c", j=PACK)
        w1_raw = [keep.tile([P, 2, H], F32, name=f"w1_raw{half}", align_bytes=64) for half in range(2)]
        scales = stage.tile([P, T], U8, name="scales", align_bytes=64, offset=SCALES_AT)
        nc.vector.memset(scales[:].bitcast(I32), 0)
        words = stage.tile([P, T], U32, name="words", align_bytes=64, offset=WORDS_AT)
        w2_rows = w2.rearrange("(g u i e) n -> u g i (e n)", u=2, i=2, e=2)
        w2_raw = [stage.tile([P, 2, N], F32, name=f"w2_raw{u}", align_bytes=64, offset=W2_RAW_AT[u]) for u in range(2)]

        nc.sync.dma_start(w1_raw[0][:], w1_rows[:, 0:2, :])
        nc.sync.dma_start(offsets[:], offs)
        for q in (0, 2, 1, 3):
            nc.sync.dma_start(scales[32 * q : 32 * q + 4, :].bitcast(I32), x_scales[0, 4 * q : 4 * q + 4, :].bitcast(I32))
        nc.sync.dma_start(w1_raw[1][:], w1_rows[:, 2:4, :])
        nc.sync.dma_start(words[:].bitcast(I32), x_words[0].rearrange("p n t -> p (n t)").bitcast(I32))
        for u in range(2):
            nc.sync.dma_start(w2_raw[u][:].rearrange("p e n -> p (e n)"), w2_rows[u])

        x_scales_early = keep.tile([P, S - CHUNK], U8, name="x_scales_early", align_bytes=64)
        nc.vector.tensor_copy(x_scales_early[:], scales[:].indirect(offsets[:, CHUNK // 16 :]))

        w1_codes = keep.tile([P, H], U32, name="w1_codes", align_bytes=64)
        w1_scales = keep.tile([P, H], U8, name="w1_scales", align_bytes=64)
        w1_bf = [stage.tile([P, 2, P * PACK], BF16, name=f"w1_bf{u}", align_bytes=64, offset=W1_BF_AT[u]) for u in range(2)]
        for half in range(2):
            columns = w1_raw[half][:].rearrange("p j (g u i e) -> p u g j i e", u=2, i=2, e=2)
            for u in (1, 0):
                dealt = w1_bf[u][:].rearrange("p e (g i j) -> p g j i e", i=2, j=PACK)[:, :, 2 * half : 2 * half + 2]
                split = SCALAR_GROUPS[half][u]
                nc.scalar.copy(dealt[:, :split], columns[:, u, :split])
                if split < GROUPS:
                    nc.vector.tensor_copy(dealt[:, split:], columns[:, u, split:])
        x_early = [stage.tile([P, CHUNK], U32, name=f"x_codes{c}", align_bytes=64, offset=X_CODES_AT[c]) for c in range(2)]
        x_late = stage.tile([P, 2 * CHUNK], U32, name="x_late", align_bytes=64, offset=X_CODES_AT[2])
        x_codes = [x_early[0][:], x_early[1][:], x_late[:, CHUNK : 2 * CHUNK], x_late[:, 0:CHUNK]]
        x_scales_last = stage.tile([P, CHUNK], U8, name="x_scales_last", align_bytes=64, offset=X_SCALES_LAST_AT)
        planes = [x_scales_early[:, (ORDER[c] - 1) * CHUNK : ORDER[c] * CHUNK] for c in range(LAST)] + [x_scales_last[:]]

        def quantize_w1(u):
            cols = slice(2 * u * P, 2 * (u + 1) * P)
            nc.vector.quantize_mx(out=w1_codes[:, cols].bitcast(FP8X4), scales=w1_scales[:, cols], in_=w1_bf[u][:].rearrange("p e n -> p (e n)"))

        def gather_words(c):
            nc.vector.tensor_copy(x_codes[c], words[:].indirect(offsets[:, ORDER[c] * (CHUNK // 16) : (ORDER[c] + 1) * (CHUNK // 16)]))

        def gather_scales(c):
            nc.vector.tensor_copy(planes[c], scales[:].indirect(offsets[:, ORDER[c] * (CHUNK // 16) : (ORDER[c] + 1) * (CHUNK // 16)]))

        quantize_w1(1)
        quantize_w1(0)
        for c in range(2):
            gather_words(c)
        nc.vector.tensor_copy(x_late[:], words[:].indirect(offsets[:, 0 : 2 * CHUNK // 16]))

        h_banks = [psum.tile([P, PACK, CHUNK], F32, name=f"h_bank{c}", tag=f"h_bank{c}") for c in range(CHUNKS)]

        def first_product(c):
            for t in (2, 3, 0, 1):
                nc.tensor.matmul_mx(
                    out=h_banks[c][:, t, :],
                    lhsT=w1_codes[:, t * P : (t + 1) * P].bitcast(FP8X4),
                    lhsT_scale=w1_scales[:, t * P : (t + 1) * P],
                    rhs=x_codes[c].bitcast(FP8X4),
                    rhs_scale=planes[c],
                    start=True,
                    stop=True,
                )

        for c in range(2):
            first_product(c)

        w2_bf = [
            keep.tile([P, N * PACK], BF16, name="w2_bf", align_bytes=64),
            keep.tile([P, N * PACK], BF16, name="w2_neg", align_bytes=64),
        ]

        def w2_views(u):
            dealt = w2_bf[0][:].rearrange("p (a l t) -> p a l t", l=4, t=PACK)[:, :, :, 2 * u : 2 * u + 2].rearrange("p a l t -> p a t l")
            return dealt, w2_raw[u][:].rearrange("p t (a l) -> p a t l", l=4)

        nc.scalar.copy(*w2_views(0))
        nc.vector.tensor_copy(*w2_views(1))
        gather_scales(LAST)
        nc.vector.tensor_scalar(w2_bf[1][:], w2_bf[0][:], -1.0, None, ALU.mult)
        w2_codes = keep.tile([P, 2 * N], U32, name="w2_codes", align_bytes=64)
        w2_scales = keep.tile([P, 2 * N], U8, name="w2_scales", align_bytes=64)

        def quantize_w2(sign):
            cols = slice(sign * N, (sign + 1) * N)
            nc.vector.quantize_mx(out=w2_codes[:, cols].bitcast(FP8X4), scales=w2_scales[:, cols], in_=w2_bf[sign][:])

        for c in range(2, CHUNKS):
            first_product(c)

        h_view = [bank[:].rearrange("p t (v d) -> p d v t", d=D) for bank in h_banks]
        h_bf = keep.tile([P, 2 * D, 2, CHUNK_QUERIES, PACK], BF16, name="h_bf", align_bytes=64)
        h_late, h_early = h_bf[:, :D], h_bf[:, D:]
        for c in range(2):
            nc.scalar.activation(h_early[:, :, c], h_view[c][:, ::-1], ACT.Relu)
        quantize_w2(0)
        quantize_w2(1)
        for c, part in ((2, slice(0, 3)), (3, slice(2, 4)), (3, slice(0, 2))):
            nc.scalar.activation(h_late[:, part, LAST - c], h_view[c][:, part], ACT.Relu)
        h_codes = keep.tile([P, S], U32, name="h_codes", align_bytes=64)
        h_scales = keep.tile([P, S], U8, name="h_scales", align_bytes=64)

        def quantize_h(source, first, count, slot):
            cols = slice(slot * SLOT, (slot + count) * SLOT)
            nc.vector.quantize_mx(
                out=h_codes[:, cols].bitcast(FP8X4),
                scales=h_scales[:, cols],
                in_=source[:, first : first + count].rearrange("p d c v t -> p (d c v t)"),
            )

        def score_pass(target, m, sign, slot, start, stop):
            cols = slice(slot * SLOT, (slot + 2) * SLOT)
            stationary = slice(sign * N + m * P, sign * N + (m + 1) * P)
            nc.tensor.matmul_mx(
                out=target,
                lhsT=w2_codes[:, stationary].bitcast(FP8X4),
                lhsT_scale=w2_scales[:, stationary],
                rhs=h_codes[:, cols].bitcast(FP8X4),
                rhs_scale=h_scales[:, cols],
                start=start,
                stop=stop,
            )

        def differences(name, plus, minus):
            bank = psum.tile([P, OUT_TILES, 2, SLOT], F32, name=name, tag=name)
            for sign, slot in enumerate((plus, minus)):
                for m in range(OUT_TILES):
                    score_pass(bank[:, m].rearrange("p a v -> p (a v)"), m, sign, slot, (sign, m) == (0, 0), (sign, m) == (1, OUT_TILES - 1))
            return bank[:].rearrange("p m a v -> p a m v")

        q12 = keep.tile([P, 4, OUT_TILES, SLOT], F32, name="q12", align_bytes=64)
        q3 = keep.tile([P, 2, OUT_TILES, SLOT], F32, name="q3", align_bytes=64)
        quantize_h(h_early, 2, 2, 4)
        quantize_h(h_early, 1, 1, 3)
        nc.vector.tensor_scalar(h_late[:, 3, 1], h_view[2][:, 3], 0.0, None, ALU.max)
        nc.scalar.activation(q12[:, 2:4], differences("early", 4, 3), ACT.Exp)
        quantize_h(h_late, 2, 1, 2)
        quantize_h(h_bf, 3, 2, 6)
        nc.scalar.activation(q3[:], differences("third", 2, 6), ACT.Exp)
        late_banks = [psum.tile([P, 2, SLOT], F32, name=f"late{m}", tag=f"late{m}") for m in range(OUT_TILES)]
        quantize_h(h_late, 0, 2, 0)
        for m in range(OUT_TILES):
            for sign in range(2):
                score_pass(late_banks[m][:].rearrange("p a v -> p (a v)"), m, sign, sign, sign == 0, sign == 1)
            nc.scalar.activation(q12[:, 0:2, m], late_banks[m][:], ACT.Exp)

        def wide(name):
            return keep.tile([P, 2, OUT_TILES * SLOT], F32, name=name, align_bytes=64)

        flat = q12[:].rearrange("p s m v -> p s (m v)")
        q1, q2 = flat[:, 0:4:3], flat[:, 1:3]
        q3_flat = q3[:].rearrange("p g m v -> p g (m v)")
        second, first, pair, third, product = [wide(name) for name in ("second", "first", "pair", "third", "product")]
        late, early = 0, 1

        def plus_one_times(target, left, right):
            nc.vector.scalar_tensor_tensor(target, left, 1.0, right, ALU.add, ALU.mult)

        for g in (early, late):
            plus_one_times(second[:, g], q1[:, g], q2[:, g])
            nc.vector.tensor_scalar(first[:, g], q1[:, g], 1.0, 2.0**-PRODUCT_SHIFT, ALU.add, ALU.mult)
            plus_one_times(third[:, g], second[:, g], q3_flat[:, g])
            plus_one_times(pair[:, g], second[:, g], first[:, g])
        for m in range(OUT_TILES):
            cols = slice(m * SLOT, (m + 1) * SLOT)
            plus_one_times(product[:, :, cols], third[:, :, cols], pair[:, :, cols])
        for m in range(OUT_TILES):
            cols = slice(m * SLOT, (m + 1) * SLOT)
            log_product = keep.tile([P, 2, SLOT], F32, name=f"log_product{m}", align_bytes=64)
            nc.scalar.activation(log_product[:], product[:, :, cols], ACT.Ln)
            result = keep.tile([P, 2, SLOT], F32, name=f"result{m}", align_bytes=64)
            nc.vector.tensor_scalar(result[:], log_product[:], PRODUCT_SHIFT * LN2, None, ALU.add)
            nc.sync.dma_start(out[m * P : (m + 1) * P, :], result[:].rearrange("p g v -> p (g v)"))
